import numpy as np, ml_dtypes
CORES = [13,21,141,149]
N = 4
BF = ml_dtypes.bfloat16
def gentries(a):
    return np.ascontiguousarray(a.reshape(8, 16, -1).transpose(0, 2, 1)).reshape(8, -1)
def gtable(e):
    e = np.asarray(e); return np.ascontiguousarray(e.reshape(8, -1, 16).transpose(0, 2, 1)).reshape(128, -1).astype(np.int32)
V, R, L, T, M = 1024, 3072, 256, 4, 2048
def parts(rng):
    rec = rng.integers(0, 256, (N, 8, 16, R)); ch = rng.integers(0, R, (N, 8, 16, V)); at = rng.integers(0, 256, (N, 8, 16, L))
    key0 = np.where(rng.random((N, 8, L)) < 0.25, rng.integers(0, V // 16, (N, 8, L)), rng.integers(0, V, (N, 8, L)))
    th = rng.integers(1650, 2000, (N, 8, 1, 1)) + rng.integers(0, 250, (N, 8, 16, 1)); w = rng.integers(0, 16, (N, 8, 16, 1))
    return rec, ch, at, key0, th, w
def pack(rec, ch, at, key0, th, w):
    return {"rec": np.ascontiguousarray(rec.reshape(N, 128, R)).astype(np.float32).astype(BF), "ch": np.ascontiguousarray(ch.reshape(N, 128, V)).astype(np.int32),
            "at": np.ascontiguousarray(at.reshape(N, 128, L)).astype(np.float32).astype(BF), "key0": np.stack([gtable(a) for a in key0]),
            "th": np.ascontiguousarray(th.reshape(N, 128, 1)).astype(np.int32), "w": np.ascontiguousarray(w.reshape(N, 128, 1)).astype(np.int32)}
def setup_inputs(rng):
    return pack(*parts(rng))
def setup_inputs_clash(rng):
    rec, ch, at, key0, th, w = parts(rng); o = rng.permutation(L)
    at[..., o[1::2]] = at[..., o[0::2]]
    key0[:, 1::2] = rng.integers(0, V, (N, 4, 8))[np.arange(N)[:, None, None], np.arange(4)[None, :, None], rng.integers(0, 8, (N, 4, L))]
    key0[:, ::2, o[1::2]] = key0[:, ::2, o[0::2]]
    one = (np.arange(16)[None, None, :, None] == rng.integers(0, 16, (N, 8, 1, 1))).astype(np.int64)
    w = np.where((rng.random((N, 8, 1, 1)) < 0.5), one, w)
    w[rng.integers(0, N - 1), rng.integers(0, 8)] = 0
    ga, gb, gc = [int(i) for i in rng.permutation(8)[:3]]
    th[0, ga] = 4080; w[0, ga] = 0; th[1, ga] = 0
    for g in (gb, gc):
        key0[:, g] = np.argsort(rng.random((N, V)), axis=1)[:, :L]; th[0, g] = 0
    key0[:, gc, L - 1] = key0[:, gc, 0]
    return pack(rec, ch, at, key0, th, w)
def setup_inputs_ends(rng):
    rec, ch, at, key0, th, w = parts(rng)
    rec = 255 * (rng.random((N, 8, 16, R)) < rng.random((N, 8, 1, R))).astype(np.int64); at = 255 * (rng.random((N, 8, 16, L)) < rng.random((N, 8, 1, L))).astype(np.int64)
    at = np.where(rng.random((N, 8, 1, L)) < 0.3, 255 * rng.integers(0, 2, (N, 8, 1, L)), at)
    th = np.minimum(th + 700, 4080)
    key0[:, ::2] = rng.choice(np.array([0, 1, V - 2, V - 1]), (N, 4, L))
    ch[:, 4] = ch[:, 4, :1]
    for g in (3, 5):
        rec[:, g] = 255 * (rng.random((N, 1, R)) < 0.1); rec[:, g, :, R - 1458:R - 1455] = 0
        at[:, g] = 255 * (rng.random((N, 1, L)) < 0.9)
        ch[:, g] = rng.choice(np.array([0, R - 1, R - 1456, R - 1457, R - 1458]), (N, 16, V))
    th[:, 3] = 4079; th[:, 5] = rng.choice(np.array([0, 4079, 4080]), (N, 16, 1))
    w[:, 1] = 15
    rec[:, 1] = np.abs(255 * (rng.random((N, 16, R)) < 0.05) - rng.integers(0, 8, (N, 16, R)))
    at[:, 1] = np.abs(255 * (rng.random((N, 16, L)) < 0.6 + 0.4 * rng.random((N, 1, L))) - rng.integers(0, 8, (N, 16, L)))
    ch[:, 1, :, V - 1] = 0; rec[:, 1, :, 0] = 0; at[:, 1, :, 0] = 255; key0[:, 1, 0] = V - 1
    s = np.arange(N)[:, None] * L + np.argsort(rng.random((N, L)), axis=1) + 1
    turn = (np.arange(16)[None, :, None] + rng.integers(0, 16, (N, 1, L))) % 16
    at[:, 7] = s[:, None, :] // 16 + (turn < s[:, None, :] % 16); key0[:, 7] = s - 1
    rec[0, 7, :, :R - M] = 255; rec[0, 7, :, R - M:] = 0; ch[0, 7, 0] = R - M - 1
    th[0, 7] = 4080; th[0, 7, 0] = 2048; w[0, 7] = 0; w[0, 7, 0] = 1; th[1, 7] = 0
    return pack(rec, ch, at, key0, th, w)
def setup_inputs_quiet(rng):
    rec, ch, at, key0, th, w = parts(rng); q = rng.permutation(N)
    th[q[0]] = 4080; th[q[1]] = 0; th[:, rng.integers(0, 8)] = 4080; w[q[2]] = 15
    return pack(rec, ch, at, key0, th, w)
def setup_inputs_spread(rng):
    rec, ch, at, key0, th, w = parts(rng)
    rec = np.minimum((np.exp2(8 * rng.random((N, 8, 1, R))) * rng.random((N, 8, 16, R))).astype(np.int64), 255)
    at = np.minimum((np.exp2(8 * rng.random((N, 8, 1, L))) * rng.random((N, 8, 16, L))).astype(np.int64), 255)
    th = np.where(rng.random((N, 8, 16, 1)) < 0.1, rng.integers(0, 4081, (N, 8, 16, 1)), rng.integers(1200, 4081, (N, 8, 16, 1)))
    w = w * (rng.random((N, 8, 16, 1)) < 0.6)
    return pack(rec, ch, at, key0, th, w)
def setup_inputs_ties(rng):
    rec, ch, at, key0, th, w = parts(rng); u = rng.permutation(np.array([1, 1, 1, 2, 7, 16, 100, 255])).reshape(1, 8, 1, 1)
    rec = u * (rng.random((N, 8, 16, R)) < rng.random((N, 8, 1, R))); at = u * (rng.random((N, 8, 16, L)) < rng.random((N, 8, 1, L)))
    th = u * rng.integers(10, 15, (N, 8, 16, 1)) - rng.integers(0, 2, (N, 8, 16, 1))
    g = int(rng.integers(0, 8)); z = 255 * rng.integers(0, 2, 16); at[:, g] = z[:, None]
    th[:2, g] = 0; w[0, g] = 0
    e1, e2 = [R // 3 + int(i) for i in rng.integers(-150, 151, 2)]; steps = [e1, e2, R - e1 - e2]
    cs = [int(rng.integers(0, 100)), int(rng.integers(100, 200)), R - 1 - int(rng.integers(0, 100))]
    rec[1, g, :, 300] = z; ch[1, g, :, 0] = 300
    places = np.sort(rng.permutation(16)[:3])
    for i in range(3):
        far = int(np.nonzero(((37 * np.arange(M) + 1) & (M - 1)) == steps[i])[0][0])
        rec[1, g, :, cs[i]] = np.abs(z - (far // 16 + (np.arange(16) < far % 16)))
        rec[1, g, :, (cs[i] + steps[i]) % R] = z
        ch[1, g, places[i], 0] = cs[i]
    rec[0, g, 0, 1:] = 255 - z[0]; rec[0, g, :, 0] = z
    ch[0, g] = np.where(np.arange(V)[None, :] % 2 == 0, 0, rng.integers(1, R, (16, V)))
    key0[:, g] = 2 * rng.integers(0, V // 2, (N, L)); key0[2:N - 1, g] += 1; key0[1, g, 0] = 0
    return pack(rec, ch, at, key0, th, w)
def check_inputs(d):
    bad = []
    for k, hi in (("rec", 255), ("ch", R - 1), ("at", 255), ("key0", V - 1), ("th", 4080), ("w", 15)):
        v = np.asarray(d[k]).astype(np.float64)
        if not np.all((v >= 0) & (v <= hi) & (v == np.floor(v))): bad.append("range of " + k)
    return bad
def reference(rec, ch, at, key0, th, w):
    x = rec.astype(np.float32).astype(np.int32).reshape(N, 8, 16, R); a = at.astype(np.float32).astype(np.int32).reshape(N, 8, 16, L)
    c0 = ch.astype(np.int32).reshape(N, 8, 16, V); c = np.array(c0); lim = th.astype(np.int32).reshape(N, 8, 16, 1); wt = w.astype(np.int32).reshape(N, 8, 16, 1)
    k0 = np.stack([gentries(q) for q in key0]).astype(np.int64)
    key = np.array(k0); mark = np.zeros((N, 8, L), bool)
    low = np.tri(L, L, -1).astype(bool)
    for t in range(T):
        for b in range(N):
            r = (b + t) % N
            if t == 0 or r == 0:
                key[b] = k0[b]; mark[b] = False
            k = np.array(key[b]); m = np.array(mark[b])
            old = np.take_along_axis(c[r], k[:, None, :], 2)
            rows = np.take_along_axis(x[r], old.reshape(8, 1, 16 * L), 2).reshape(8, 16, 16, L)
            d = np.add.reduce(np.abs(rows - a[b][:, :, None, :]), axis=1)
            fail = d > lim[r]; bad = np.any(fail, axis=1); first = np.argmax(fail, axis=1)
            step = old + ((37 * d + 1) & (M - 1)); step = np.where(step >= R, step - R, step)
            mended = np.where(np.arange(16)[None, :, None] == first[:, None, :], step, old)
            back = np.take_along_axis(c0[r], k[:, None, :], 2)
            col = np.where(m[:, None, :], back, mended)
            want = m | bad
            lost = np.any((k[:, :, None] == k[:, None, :]) & want[:, None, :] & low[None], axis=2)
            win = want & ~lost
            for g in range(8):
                jj = np.nonzero(win[g])[0]
                c[r, g][:, k[g, jj]] = col[g][:, jj]
            mark[b] = m | win
            key[b] = np.add.reduce(wt[r] * d, axis=1) & (V - 1)
    end = [(r - (T - 1)) % N for r in range(N)]
    return {"yc": c.reshape(N, 128, V).astype(np.float32), "yk": np.stack([key[b] + V * mark[b] for b in end]).astype(np.float32)}

@@ -1,0 +1,519 @@
+from concourse.mybir import AluOpType as ALU, ActivationFunctionType as ACT
+
+N, V, R, L, NT = 4, 1024, 3072, 256, 4
+CFG = {
+    "stages": [(0, 128), (128, 192), (192, 256)],
+    "gat": [(e, 32 * i, 32 * i + 32) for i, e in enumerate("vssvvvsv")],
+    "abs": [(c, c + 1) for c in range(8)],
+    "red": [(0, 64), (64, 128), (128, 192), (192, 256)],
+    "old": [(0, 32), (32, 64), (64, 128), (128, 192), (192, 256)],
+    "hop": 5000.0, "lat": 100.0, "slack": 0.0, "gam": 1.56, "pe": 0.52, "cy": 1.04,
+    "t1": "vvvv",
+}
+MAXS = 4
+
+SCRATCH = {}
+for _dt, _bufs in (
+    ("bfloat16", dict(rec_s=R, at_s=L, nat=4 * L, ones=128, ident=128, g1=128, gg=128, lw=128, tmpa=128, tmpb=128, t18=128,
+                      ni18=128, tz=128, g20=128, gn=128, bsel=144, ex=2048, dm=L, cq=L, cz=L, rq=L, rz=L, xg=16 * L,
+                      ab=16 * L, eq=16 * L, mb=L, fail=L)),
+    ("float16", dict(id16=128, w16=128, kb=L, dh=L, mo16=16)),
+    ("int32", dict(ch_s=V, k0_s=16, th_s=4, w_s=4, di=L, d16=16, uu=L, ee=L, ki=16, kj=16)),
+    ("uint16", dict(k0u=16, mi=96, mo=96, coff=L, soff=16)),
+    ("float32", dict(thf=4, wf=4, win=256 + 2 * V, iow=2 * V, key3=16, mneg=16, wantv=16, t1=L, st=L, tw=L, sq=L, sz=L,
+                     mk1=16, mk2=16, mof=16, ykb=L)),
+):
+    for _k, _n in _bufs.items():
+        SCRATCH[_k] = ("sbuf", [128, _n], _dt)
+PSUM = dict(py=2048, pd0=512, pd1=512, pq=512, pz=512)
+for _k, _n in PSUM.items():
+    SCRATCH[_k] = ("psum", [128, _n], "float32")
+SEMAPHORES = (["qv", "qs", "qt", "qg", "sent", "a0", "a1", "a2", "a3", "k0"]
+              + ["m%d_%d" % (t, s) for t in range(NT - 1) for s in range(MAXS)]
+              + ["l_at", "l_k0", "l_th", "l_w", "l_ch", "l_c1", "l_r0", "l_r1", "o_c0", "o_c1", "o_k"])
+
+
+def helper_of(T, topo, r):
+    c, nxt = T.cores[r], T.cores[(r + 1) % N]
+    ok = [h for h in topo.cores_of(c) if h != c and topo.may_write(h, nxt)]
+    near = [h for h in ok if topo.die(h) == topo.die(c)]
+    return (near or ok)[0]
+
+
+def nmask(topo, a, b):
+    return len(topo.engines(a, b))
+
+
+def rsend(g, T, topo, src, dst, out_ap, in_ap, sem):
+    rid, pid = topo.addr(dst, src)
+    g.remote_dma(out_ap, in_ap, T.sem[sem], T.sem["sent"], pid, rid, topo.mask(src, dst))
+    return nmask(topo, src, dst)
+
+
+def msg_cols(t, s):
+    st = CFG["stages"]
+    return 32 * t + st[s][0] // 16, 32 * t + (32 if s == len(st) - 1 else st[s][1] // 16)
+
+
+def helper_program(g, core, T, topo, r):
+    me = T.cores[r]
+    n_in = nmask(topo, me, core)
+    sent = 0
+    g.wait_ge(T.sem["a0"], n_in)
+    sent += rsend(g, T, topo, core, T.cores[(r + 1) % N], T.nat[:, L:2 * L], T.nat[:, 0:L], "a1")
+    if not topo.may_write(me, T.cores[0]) and r != 0:
+        t = (0 - r) % N
+        g.wait_ge(T.sem["k0"], n_in)
+        sent += rsend(g, T, topo, core, T.cores[0], T.mi[:, 32 * (t - 1):32 * (t - 1) + 16], T.k0u[:, 0:16], "m%d_0" % (t - 1))
+    sent += rsend(g, T, topo, core, T.cores[(r + 3) % N], T.nat[:, 3 * L:4 * L], T.nat[:, 0:L], "a3")
+    if r < N - 1:
+        for t in range(NT - 1):
+            for s in range(len(CFG["stages"])):
+                c0, c1 = msg_cols(t, s)
+                g.wait_ge(T.sem["m%d_%d" % (t, s)], n_in)
+                sent += rsend(g, T, topo, core, T.cores[r + 1], T.mi[:, c0:c1], T.mi[:, c0:c1], "m%d_%d" % (t, s))
+    g.wait_ge(T.sem["sent"], sent)
+
+
+def rank_program(g, core, T, topo):
+    rank = T.rank_of(core)
+    if rank is None:
+        for r in range(N):
+            if helper_of(T, topo, r) == core:
+                helper_program(g, core, T, topo, r)
+        return
+    STAGES = CFG["stages"]
+    NS = len(STAGES)
+    CY, GAM, LAT = CFG["cy"], CFG["gam"], CFG["lat"]
+    hlp = helper_of(T, topo, rank)
+    ops = []
+    sent = [0]
+    mark = {}
+
+    def A(name, lo, hi, step=1, p1=128):
+        ap = T[name][0:p1, lo:hi:step] if step != 1 else T[name][0:p1, lo:hi]
+        return (ap, (name, lo, hi, step))
+
+    def IND(w, o):
+        return (w[0].indirect(o[0]), w[1], o[1])
+
+    def regs(xs):
+        out = []
+        for x in xs:
+            if isinstance(x, tuple):
+                out.extend(x[1:])
+        return out
+
+    def val(x):
+        return x[0] if isinstance(x, tuple) else x
+
+    def nel(x):
+        r_ = x[-1]
+        n = (r_[2] - r_[1] + r_[3] - 1) // r_[3]
+        return 16 * n if len(x) == 3 else n
+
+    def two(x):
+        return SCRATCH[x[1][0]][2] in ("bfloat16", "float16", "uint16")
+
+    def add(q, fn, rd, wr, cost, sem=None, done=None):
+        ops.append({"q": q, "fn": fn, "rd": regs(rd), "wr": regs(wr), "sem": sem, "inc": False, "cost": cost,
+                    "done": done, "soft": []})
+        return len(ops) - 1
+
+    def vcost(o, i, per=None):
+        if len(i) == 3:
+            return 50 + nel(i) * GAM * CY
+        if per is None:
+            per = 0.5 if two(o) and two(i) else 1.0
+        return max(64, nel(o) * per) * CY
+
+    def vcopy(o, i):
+        return add("v", lambda: g.vector.tensor_copy(o[0], i[0]), [i], [o], vcost(o, i))
+
+    def vts(o, i, s1, s2, op0, op1=None):
+        if op1 is None:
+            return add("v", lambda: g.vector.tensor_scalar(o[0], i[0], val(s1), None, op0), [i, s1], [o], vcost(o, i))
+        return add("v", lambda: g.vector.tensor_scalar(o[0], i[0], val(s1), val(s2), op0, op1), [i, s1, s2], [o], vcost(o, i))
+
+    def vtt(o, a, b, op):
+        if len(o) == 3:
+            return add("v", lambda: g.vector.tensor_tensor(o[0], a[0], b[0], op), [a, b, (None, o[2])], [(None, o[1])],
+                       50 + nel(o) * 3.8 * CY)
+        per = 1.0 if a[1][0] in PSUM or b[1][0] in PSUM else 2.0
+        return add("v", lambda: g.vector.tensor_tensor(o[0], a[0], b[0], op), [a, b], [o], vcost(o, a, per))
+
+    def vset(o, c):
+        return add("v", lambda: g.vector.memset(o[0], c), [], [o], vcost(o, o))
+
+    def vscan(o, d0, d1, init):
+        return add("v", lambda: g.vector.tensor_tensor_scan(o[0], d0[0], d1[0], init, ALU.min, ALU.max), [d0, d1], [o],
+                   vcost(o, d1))
+
+    def act(o, i, f, bias=None, scale=1.0):
+        cost = 65 + nel(i) * (GAM if len(i) == 3 else 1.0) * CY
+        if bias is not None:
+            return add("s", lambda: g.scalar.activation(o[0], i[0], f, bias=bias, scale=scale), [i], [o], cost)
+        return add("s", lambda: g.scalar.activation(o[0], i[0], f), [i], [o], cost)
+
+    def mm(o, lh, rh, start, stop):
+        return add("t", lambda: g.tensor.matmul(o[0], lh[0], rh[0], start, stop), [lh, rh], [o],
+                   max(min(64, nel(lh)), nel(rh)) * CFG["pe"])
+
+    def dma(q, o, i, sem, done):
+        eng = g.sync if q == "y" else g.scalar
+        return add(q, lambda: eng.dma_start(val(o), val(i)), [i], [o], 60, (sem, 16), done)
+
+    def send(dst, out_ap, i, sem):
+        sent[0] += nmask(topo, core, dst)
+        return add("g", lambda: rsend(g, T, topo, core, dst, out_ap, i[0], sem), [i], [], 300, "remote")
+
+    def M(name):
+        return A(name, 0, 128)
+
+    dma("y", A("at_s", 0, L), T.at[:], "l_at", 2200)
+    dma("s", A("k0_s", 0, 16), T.key0[:], "l_k0", 2300)
+    dma("y", A("ch_s", 0, V // 2), T.ch[:, 0:V // 2], "l_ch", 4300)
+    dma("s", A("ch_s", V // 2, V), T.ch[:, V // 2:V], "l_c1", 4300)
+    dma("y", A("rec_s", 0, R // 2), T.rec[:, 0:R // 2], "l_r0", 7300)
+    dma("s", A("rec_s", R // 2, R), T.rec[:, R // 2:R], "l_r1", 7300)
+    dma("y", A("th_s", 0, 1), T.th[:], "l_th", 8000)
+    dma("s", A("w_s", 0, 1), T.w[:], "l_w", 8000)
+    n_loads = len(ops)
+
+    def sel(o, i, pat, op, base, cm):
+        add("g", lambda: g.affine_select(o[0], i[0], pat, op, 0.0, base, cm), [i], [o], 210 + 2 * CY * nel(o))
+
+    def iota(o, pat, base, cm, small=False):
+        if small:
+            add("g", lambda: g.iota(o[0], pat, base, cm, allow_small_or_imprecise_dtypes=True), [], [o], 160 + 2 * CY * nel(o))
+        else:
+            add("g", lambda: g.iota(o[0], pat, base, cm), [], [o], 160 + 2 * CY * nel(o))
+
+    vset(M("ones"), 1.0)
+    sel(M("ident"), M("ones"), [[-1, 128]], ALU.is_equal, 0, 1)
+    sel(M("g1"), M("ones"), [[-16, 8], [0, 16]], ALU.is_ge, 0, 1)
+    sel(M("gg"), M("g1"), [[16, 8], [0, 16]], ALU.is_ge, 15, -1)
+    iota(A("di", 0, L), [[0, 16], [-1, 16]], 16, 1)
+    sel(M("lw"), M("gg"), [[1, 128]], ALU.is_gt, 0, -1)
+    iota(A("d16", 0, 16), [[1, 16]], 0, 16)
+    vset(A("iow", V, 2 * V), 2047.0)
+    vset(A("win", 0, 256), 0.0)
+    vset(A("bsel", 0, 144), 0.0)
+    vset(A("rq", 0, L), float(2 ** 27))
+    vset(A("rz", 0, L), 4096.0)
+    vset(A("rq", 0, L, 16), -float(2 ** 27))
+    for h in range(2):
+        mm(A("pq", 128 * h, 128 * h + 128), A("at_s", 128 * h, 128 * h + 128), M("ident"), True, True)
+    for i in range(16):
+        if i % 2 == 0:
+            act(A("ex", i, 2048, 16), M("ident"), ACT.Copy)
+        else:
+            vcopy(A("ex", i, 2048, 16), M("ident"))
+    vts(A("nat", 0, L), A("pq", 0, L), -1.0, None, ALU.mult)
+    vcopy(A("k0u", 0, 16), A("k0_s", 0, 16))
+    first = [send(hlp, T.nat[:, 0:L], A("nat", 0, L), "a0")]
+    if rank != 0:
+        t = (0 - rank) % N
+        if topo.may_write(core, T.cores[0]):
+            first.append(send(T.cores[0], T.mi[:, 32 * (t - 1):32 * (t - 1) + 16], A("k0u", 0, 16), "m%d_0" % (t - 1)))
+        else:
+            first.append(send(hlp, T.k0u[:, 0:16], A("k0u", 0, 16), "k0"))
+    first.append(send(T.cores[(rank + 2) % N], T.nat[:, 2 * L:3 * L], A("nat", 0, L), "a2"))
+    iota(A("iow", 0, V), [[1, V]], 0, 0, True)
+    vcopy(A("bsel", 15, 128, 16), A("gg", 0, 128, 16))
+    vts(A("di", 0, L), A("di", 0, L), 15, None, ALU.bitwise_and)
+    vts(A("d16", 0, 16), A("d16", 0, 16), 255, None, ALU.bitwise_and)
+    vtt(M("tmpa"), M("ident"), M("lw"), ALU.subtract)
+    vts(A("dm", 0, L), A("di", 0, L), 0.0, None, ALU.is_equal)
+    vts(A("rz", 0, L, 16), A("d16", 0, 16), -1.0, 255.0, ALU.mult, ALU.add)
+    vtt(M("tmpb"), M("tmpa"), M("lw"), ALU.subtract)
+    vts(M("t18"), M("tmpa"), float(2 ** 18), None, ALU.mult)
+    vts(A("cq", 0, L), A("dm", 0, L), float(2 ** 26 - 2 ** 19), -float(2 ** 26), ALU.mult, ALU.add)
+    vts(A("cz", 0, L), A("dm", 0, L), 8192.0 - 1792.0, -8192.0, ALU.mult, ALU.add)
+    vts(M("tz"), M("tmpb"), 2048.0, None, ALU.mult)
+    vts(M("ni18"), M("ident"), -float(2 ** 18), None, ALU.mult)
+    vts(M("g20"), M("gg"), float(2 ** 20), None, ALU.mult)
+    vts(M("gn"), M("gg"), -4096.0, None, ALU.mult)
+    vcopy(M("id16"), M("ident"))
+    vcopy(A("win", 256, 256 + V), A("ch_s", 0, V))
+    if rank != 0:
+        act(A("win", 256 + V, 256 + 2 * V), A("win", 256, 256 + V), ACT.Identity, bias=float(R))
+    vcopy(A("wf", 0, 1), A("w_s", 0, 1))
+    vts(A("thf", 0, 1), A("th_s", 0, 1), -2048.0, None, ALU.add)
+    vts(M("w16"), M("gg"), A("wf", 0, 1), None, ALU.mult)
+
+    def ext(sem, cnt, wr):
+        return add("x", None, [], wr, 0, (sem, cnt), 0)
+
+    n_far = nmask(topo, helper_of(T, topo, (rank - 1) % N), core)
+    for k, n_ in ((1, n_far), (2, nmask(topo, T.cores[(rank + 2) % N], core)),
+                  (3, nmask(topo, helper_of(T, topo, (rank + 1) % N), core))):
+        ops[ext("a%d" % k, n_, [A("nat", k * L, k * L + L)])]["soft"].append((first[0], 6000))
+
+    def arrivals(t):
+        if rank == 0:
+            b = (0 - (t + 1)) % N
+            src = T.cores[b] if topo.may_write(T.cores[b], core) else helper_of(T, topo, b)
+            ops[ext("m%d_0" % t, nmask(topo, src, core), [A("mi", 32 * t, 32 * t + 16)])]["soft"].append((first[1], 6000))
+        else:
+            for s in range(NS):
+                c0, c1 = msg_cols(t, s)
+                ops[ext("m%d_%d" % (t, s), n_far, [A("mi", c0, c1)])]["soft"].append((mark[(t, s)], CFG["hop"]))
+
+    TAB = A("win", 256, 256 + V)
+
+    def one_round(t):
+        fresh = t == 0 or rank == 0
+        last = t == NT - 1
+        passes = last or rank < N - 1
+
+        def koff(l0, l1):
+            return A("k0u", l0 // 16, l1 // 16) if t == 0 else A("mi", 32 * (t - 1) + l0 // 16, 32 * (t - 1) + l1 // 16)
+
+        def moff(l0, l1):
+            return A("mi", 32 * (t - 1) + 16 + l0 // 16, 32 * (t - 1) + 16 + l1 // 16)
+
+        def pd(s, l0, l1):
+            return A("pd%d" % ((NS * t + s) % 2), l0, l1)
+
+        for l0, l1 in CFG["old"]:
+            vcopy(A("coff", l0, l1), IND(A("ch_s", 0, V) if t == 0 else TAB, koff(l0, l1)))
+        vcopy(A("key3", 0, 16), koff(0, L))
+        vcopy(A("kb", 0, L), IND(A("iow", 0, V), koff(0, L)))
+        if not fresh:
+            vts(A("mneg", 0, 16), moff(0, L), 1024.0, -float(2 ** 21), ALU.is_ge, ALU.mult)
+            act(A("mb", 0, L), IND(A("iow", 0, 2 * V), moff(0, L)), ACT.Relu, bias=-float(V - 1))
+        for e, l0, l1 in CFG["gat"]:
+            src = IND(A("rec_s", 0, R), A("coff", l0, l1))
+            if e == "v":
+                vcopy(A("xg", 16 * l0, 16 * l1), src)
+            else:
+                act(A("xg", 16 * l0, 16 * l1), src, ACT.Copy)
+
+        def stage(s):
+            l0, l1 = STAGES[s]
+            b0, b1 = l0 // 16, l1 // 16
+            fin = s == NS - 1
+            vts(A("dh", l0, l1), pd(s, l0, l1), -2048.0, None, ALU.add)
+            vts(A("fail", l0, l1), A("dh", l0, l1), A("thf", 0, 1), None, ALU.is_gt)
+            if CFG["t1"][s] == "v":
+                vts(A("t1", l0, l1), A("dh", l0, l1), 37.0, float(37 * 2048 + 1), ALU.mult, ALU.add)
+            else:
+                act(A("t1", l0, l1), pd(s, l0, l1), ACT.Identity, bias=1.0, scale=37.0)
+            q = A("pq", 256 + l0, 256 + l1)
+            mm(q, M("ident"), A("cq", l0, l1), True, False)
+            mm(q, M("w16"), A("dh", l0, l1), False, False)
+            mm(q, M("g20"), A("fail", l0, l1), False, True)
+            z = pd(s, 256 + l0, 256 + l1)
+            if fresh:
+                mm(z, M("t18"), A("fail", l0, l1), True, True)
+            else:
+                mm(z, M("ni18"), A("mb", l0, l1), True, False)
+                mm(z, M("t18"), A("fail", l0, l1), False, True)
+            mark[(t, s)] = vscan(A("sq", l0, l1), A("rq", l0, l1), q, 0.0)
+            vtt(A("uu", l0, l1), z, A("t1", l0, l1), ALU.min)
+            if fresh:
+                vts(A("wantv", b0, b1), A("sq", l0 + 15, l1, 16), 0.0, None, ALU.is_gt)
+            else:
+                vtt(A("wantv", b0, b1), A("sq", l0 + 15, l1, 16), A("mneg", b0, b1), ALU.is_gt)
+            if passes and (fin or not last):
+                k0 = 0 if last else b0
+                vcopy(A("ki", k0, b1), A("sq", 16 * k0 + 15, l1, 16))
+                vts(A("kj", k0, b1), A("ki", k0, b1), V - 1, None, ALU.bitwise_and)
+                if not last:
+                    vcopy(A("mo", 32 * t + b0, 32 * t + b1), A("kj", b0, b1))
+                    if not fin:
+                        c0, c1 = msg_cols(t, s)
+                        mark[(t, s)] = send(hlp, T.mi[:, c0:c1], A("mo", c0, c1), "m%d_%d" % (t, s))
+            vts(A("ee", l0, l1), A("uu", l0, l1), 2047, None, ALU.bitwise_and)
+            vtt(A("st", l0, l1), IND(TAB, koff(l0, l1)) if fresh else IND(A("win", 256, 256 + 2 * V), moff(l0, l1)),
+                A("ee", l0, l1), ALU.add)
+            vts(A("tw", l0, l1), A("st", l0, l1), float(R), -float(R), ALU.is_ge, ALU.mult)
+            z = A("pz", l0, l1)
+            mm(z, M("ident"), A("cz", l0, l1), True, False)
+            mm(z, M("id16"), A("kb", l0, l1), False, False)
+            for b in range(b0):
+                mm(z, M("gn"), A("eq", L * b + l0, L * b + l1), False, False)
+            for b in range(b0, b1):
+                vts(A("eq", L * b + 16 * b, L * b + L), A("kb", 16 * b, L), A("key3", b, b + 1), A("wantv", b, b + 1),
+                    ALU.is_equal, ALU.mult)
+                e = 16 * b + 16
+                mm(A("pz", 16 * b, e), M("tz"), A("eq", L * b + 16 * b, L * b + e), False, e == l1)
+                if e < l1:
+                    mm(A("pz", e, l1), M("gn"), A("eq", L * b + e, L * b + l1), False, False)
+            zs = vscan(A("sz", l0, l1), A("rz", l0, l1), z, 4096.0)
+            vcopy(A("soff", b0, b1), A("sz", l0 + 15, l1, 16))
+            vtt(IND(A("win", 0, 256 + V), A("soff", b0, b1)), A("st", l0, l1), A("tw", l0, l1), ALU.add)
+            if fin:
+                mark[(t, s)] = zs
+            if fin and passes:
+                if not fresh:
+                    vtt(A("mk1", 0, 16), A("sz", 15, L, 16), A("mneg", 0, 16), ALU.subtract)
+                vts(A("mk2", 0, 16), A("sz", 15, L, 16) if fresh else A("mk1", 0, 16), 256.0, 1024.0, ALU.is_ge, ALU.mult)
+                vtt(A("mo16" if last else "mof", 0, 16), A("mk2", 0, 16), A("kj", 0, 16), ALU.add)
+                if not last:
+                    vcopy(A("mo", 32 * t + 16, 32 * t + 32), A("mof", 0, 16))
+                    c0, c1 = msg_cols(t, s)
+                    mark[(t, s)] = send(hlp, T.mi[:, c0:c1], A("mo", c0, c1), "m%d_%d" % (t, s))
+
+        for c0, c1 in CFG["abs"]:
+            for c in range(c0, c1):
+                o = A("py", 512 * (c % 4), 512 * (c % 4) + 512)
+                h = c // 4
+                mm(o, A("nat", L * t + 128 * h, L * t + 128 * h + 128), A("ex", 512 * (c % 4), 512 * (c % 4) + 512), True, False)
+                mm(o, M("ident"), A("xg", 512 * c, 512 * c + 512), False, True)
+            act(A("ab", 512 * c0, 512 * c1), A("py", 512 * (c0 % 4), 512 * (c0 % 4) + 512 * (c1 - c0)), ACT.Abs)
+            for l0, l1 in CFG["red"]:
+                if 32 * c0 < l1 <= 32 * c1:
+                    s = [k for k in range(NS) if STAGES[k][0] <= l0 < STAGES[k][1]][0]
+                    for i in range(16):
+                        mm(pd(s, l0, l1), A("bsel", 15 - i, 15 - i + 128), A("ab", 16 * l0 + i, 16 * l1, 16), i == 0, i == 15)
+                    if l1 == STAGES[s][1]:
+                        stage(s)
+        if not last:
+            arrivals(t)
+
+    for t in range(NT):
+        one_round(t)
+
+    dma("y", T.yc[:, 0:V // 2], A("win", 256, 256 + V // 2), "o_c0", 3500)
+    dma("s", T.yc[:, V // 2:V], A("win", 256 + V // 2, 256 + V), "o_c1", 3500)
+    for a in range(16):
+        mm(A("pq", a, L, 16, 8), A("id16", a, 128, 16), A("mo16", 0, 16), True, True)
+    vcopy(A("ykb", 0, L, 1, 8), A("pq", 0, L, 1, 8))
+    dma("y", T.yk[:], A("ykb", 0, L, 1, 8), "o_k", 2200)
+
+    def exact(a, b):
+        if a[1] >= b[2] or b[1] >= a[2]:
+            return False
+        return not (a[3] == b[3] and (a[1] - b[1]) % a[3] != 0)
+
+    def bank(a, b):
+        return a[1] // 512 <= (b[2] - 1) // 512 and b[1] // 512 <= (a[2] - 1) // 512
+
+    wrs, rds = {}, {}
+    for n, o in enumerate(ops):
+        hard, order = set(), set()
+        for a, writes in [(x, False) for x in o["rd"]] + [(x, True) for x in o["wr"]]:
+            ps = a[0] in PSUM
+            for m, b in wrs.get(a[0], []) + (rds.get(a[0], []) if writes or ps else []):
+                p = ops[m]
+                if p["q"] == "t" and o["q"] == "t":
+                    if ps and bank(a, b):
+                        order.add(m)
+                elif ps and p["q"] != o["q"]:
+                    if bank(a, b):
+                        hard.add(m)
+                elif exact(a, b) and (writes or b in p["wr"]):
+                    hard.add(m)
+        if n < n_loads or o["q"] == "g":
+            order.update(m for m in range(n) if ops[m]["q"] == o["q"])
+        o["hard"], o["order"] = hard, order
+        if o["sem"] != "remote":
+            for a in o["wr"]:
+                for tab in (wrs, rds):
+                    if a[0] in PSUM:
+                        lo, hi = a[1] // 512 * 512, (a[2] + 511) // 512 * 512
+                        tab[a[0]] = [e for e in tab.get(a[0], []) if not (lo <= e[1][1] and e[1][2] <= hi)]
+                    elif a[3] == 1:
+                        tab[a[0]] = [e for e in tab.get(a[0], []) if not (a[1] <= e[1][1] and e[1][2] <= a[2])]
+                wrs.setdefault(a[0], []).append((n, a))
+            for a in o["rd"]:
+                rds.setdefault(a[0], []).append((n, a))
+
+    def span(p):
+        return p["cost"] if p["done"] is None else p["done"]
+
+    succ = [[] for _ in ops]
+    left = [0] * len(ops)
+    for n, o in enumerate(ops):
+        o["pre"] = ([(m, span(ops[m]) + LAT) for m in o["hard"]] + [(m, ops[m]["cost"]) for m in o["order"]]
+                    + [(m, d) for m, d in o["soft"]])
+        for m, d in o["pre"]:
+            succ[m].append((n, d))
+        left[n] = len(o["pre"])
+    prio = [0.0] * len(ops)
+    for n in range(len(ops) - 1, -1, -1):
+        prio[n] = max([span(ops[n])] + [d + prio[k] for k, d in succ[n]])
+        if rank == 0 and ops[n]["sem"] == "remote" and n + 40 < len(ops):
+            prio[n] = max(prio[n + 1:n + 40]) + 500
+    ready = [0.0] * len(ops)
+    free = {}
+    pool = {}
+    for n in range(len(ops)):
+        if left[n] == 0:
+            pool.setdefault(ops[n]["q"], []).append(n)
+    seq = []
+    while len(seq) < len(ops):
+        best = None
+        for q, c in pool.items():
+            if not c:
+                continue
+            t0 = max(free.get(q, 0.0), min(ready[n] for n in c))
+            n = max((k for k in c if ready[k] <= t0 + CFG["slack"]), key=lambda k: (prio[k], -k))
+            t1 = max(t0, ready[n])
+            if best is None or t1 < best[0]:
+                best = (t1, q, n)
+        t1, q, n = best
+        pool[q].remove(n)
+        free[q] = t1 + ops[n]["cost"]
+        seq.append(n)
+        for k, d in succ[n]:
+            ready[k] = max(ready[k], t1 + d)
+            left[k] -= 1
+            if left[k] == 0:
+                pool.setdefault(ops[k]["q"], []).append(k)
+
+    pos = {}
+    for n in seq:
+        o = ops[n]
+        o["key"] = o["q"] if o["sem"] is None or o["sem"] == "remote" else o["sem"][0]
+        pos[o["key"]] = pos.get(o["key"], 0) + 1
+        o["pos"] = pos[o["key"]]
+    seen = {}
+    for n in seq:
+        o = ops[n]
+        known = seen.setdefault(o["q"], {})
+        top = {}
+        for m in o["hard"]:
+            p = ops[m]
+            if p["key"] not in top or ops[top[p["key"]]]["pos"] < p["pos"]:
+                top[p["key"]] = m
+        need = []
+        for m in sorted(top.values(), key=lambda k: -len(ops[k]["clock"])):
+            p = ops[m]
+            if known.get(p["key"], 0) < p["pos"]:
+                need.append(m)
+                p["inc"] = True
+                known[p["key"]] = p["pos"]
+                for k_, v_ in p["clock"].items():
+                    known[k_] = max(known.get(k_, 0), v_)
+        o["need"] = need
+        o["clock"] = dict(known)
+    count = {}
+    for n in seq:
+        o = ops[n]
+        if o["sem"] is None and o["inc"]:
+            count[o["q"]] = count.get(o["q"], 0) + 1
+            o["n"] = count[o["q"]]
+    queue = {"v": g.vector, "s": g.scalar, "t": g.tensor, "g": g, "y": g.sync}
+    for n in seq:
+        o = ops[n]
+        if o["q"] == "x":
+            continue
+        for m in o["need"]:
+            p = ops[m]
+            if p["sem"] is None:
+                queue[o["q"]].wait_ge(T.sem["q" + p["q"]], p["n"])
+            else:
+                queue[o["q"]].wait_ge(T.sem[p["sem"][0]], p["sem"][1])
+        ins = o["fn"]()
+        if o["sem"] is None:
+            if o["inc"]:
+                ins.then_inc(T.sem["q" + o["q"]], 1)
+        elif o["sem"] != "remote":
+            ins.then_inc(T.sem[o["sem"][0]], 16)
+    g.wait_ge(T.sem["sent"], sent[0])
+    for o in ops:
+        if o["sem"] is not None and o["sem"] != "remote" and not o["inc"]:
+            g.wait_ge(T.sem[o["sem"][0]], o["sem"][1])

@@ -7,21 +7,21 @@ CFG = {
     "abs": [(c, c + 1) for c in range(8)],
     "red": [(0, 64), (64, 128), (128, 192), (192, 256)],
     "old": [(0, 32), (32, 64), (64, 128), (128, 192), (192, 256)],
-    "hop": 5000.0, "lat": 100.0, "slack": 0.0, "gam": 1.56, "pe": 0.52, "cy": 1.04,
-    "t1": "vvvv",
+    "hop": 7000.0, "lat": 200.0, "slack": 0.0, "gam": 1.56, "pe": 0.52, "cy": 0.9,
+    "fl": "vsss", "t1": "vsss",
 }
-MAXS = 4
+MAXS = 5
 
 SCRATCH = {}
 for _dt, _bufs in (
     ("bfloat16", dict(rec_s=R, at_s=L, nat=4 * L, ones=128, ident=128, g1=128, gg=128, lw=128, tmpa=128, tmpb=128, t18=128,
-                      ni18=128, tz=128, g20=128, gn=128, bsel=144, ex=2048, dm=L, cq=L, cz=L, rq=L, rz=L, xg=16 * L,
-                      ab=16 * L, eq=16 * L, mb=L, fail=L)),
+                      ni18=128, t18h=128, g20h=128, tz=128, g20=128, gn=128, bsel=144, ex=2048, dm=L, cq=L, cz=L, rq=L,
+                      rz=L, xg=16 * L, ab=16 * L, eq=16 * L, mb=L, fail=L)),
     ("float16", dict(id16=128, w16=128, kb=L, dh=L, mo16=16)),
     ("int32", dict(ch_s=V, k0_s=16, th_s=4, w_s=4, di=L, d16=16, uu=L, ee=L, ki=16, kj=16)),
     ("uint16", dict(k0u=16, mi=96, mo=96, coff=L, soff=16)),
-    ("float32", dict(thf=4, wf=4, win=256 + 2 * V, iow=2 * V, key3=16, mneg=16, wantv=16, t1=L, st=L, tw=L, sq=L, sz=L,
-                     mk1=16, mk2=16, mof=16, ykb=L)),
+    ("float32", dict(thf=4, tb=4, wf=4, win=256 + 2 * V, iow=2 * V, key3=16, mneg=16, wantv=16, t1=L, st=L, tw=L, sq=L,
+                     sz=L, mk1=16, mk2=16, mof=16, ykb=L)),
 ):
     for _k, _n in _bufs.items():
         SCRATCH[_k] = ("sbuf", [128, _n], _dt)
@@ -52,7 +52,10 @@ def rsend(g, T, topo, src, dst, out_ap, in_ap, sem):
 
 def msg_cols(t, s):
     st = CFG["stages"]
-    return 32 * t + st[s][0] // 16, 32 * t + (32 if s == len(st) - 1 else st[s][1] // 16)
+    cut = 16 + st[-1][0] // 16
+    if s == len(st):
+        return 32 * t + cut, 32 * t + 32
+    return 32 * t + st[s][0] // 16, 32 * t + (cut if s == len(st) - 1 else st[s][1] // 16)
 
 
 def helper_program(g, core, T, topo, r):
@@ -68,7 +71,7 @@ def helper_program(g, core, T, topo, r):
     sent += rsend(g, T, topo, core, T.cores[(r + 3) % N], T.nat[:, 3 * L:4 * L], T.nat[:, 0:L], "a3")
     if r < N - 1:
         for t in range(NT - 1):
-            for s in range(len(CFG["stages"])):
+            for s in range(len(CFG["stages"]) + 1):
                 c0, c1 = msg_cols(t, s)
                 g.wait_ge(T.sem["m%d_%d" % (t, s)], n_in)
                 sent += rsend(g, T, topo, core, T.cores[r + 1], T.mi[:, c0:c1], T.mi[:, c0:c1], "m%d_%d" % (t, s))
@@ -152,7 +155,7 @@ def rank_program(g, core, T, topo):
     def act(o, i, f, bias=None, scale=1.0):
         cost = 65 + nel(i) * (GAM if len(i) == 3 else 1.0) * CY
         if bias is not None:
-            return add("s", lambda: g.scalar.activation(o[0], i[0], f, bias=bias, scale=scale), [i], [o], cost)
+            return add("s", lambda: g.scalar.activation(o[0], i[0], f, bias=val(bias), scale=scale), [i, bias], [o], cost)
         return add("s", lambda: g.scalar.activation(o[0], i[0], f), [i], [o], cost)
 
     def mm(o, lh, rh, start, stop):
@@ -228,7 +231,7 @@ def rank_program(g, core, T, topo):
     vts(A("rz", 0, L, 16), A("d16", 0, 16), -1.0, 255.0, ALU.mult, ALU.add)
     vtt(M("tmpb"), M("tmpa"), M("lw"), ALU.subtract)
     vts(M("t18"), M("tmpa"), float(2 ** 18), None, ALU.mult)
-    vts(A("cq", 0, L), A("dm", 0, L), float(2 ** 26 - 2 ** 19), -float(2 ** 26), ALU.mult, ALU.add)
+    vts(A("cq", 0, L), A("dm", 0, L), float(2 ** 26 + 15 * 2 ** 19), -float(2 ** 26), ALU.mult, ALU.add)
     vts(A("cz", 0, L), A("dm", 0, L), 8192.0 - 1792.0, -8192.0, ALU.mult, ALU.add)
     vts(M("tz"), M("tmpb"), 2048.0, None, ALU.mult)
     vts(M("ni18"), M("ident"), -float(2 ** 18), None, ALU.mult)
@@ -239,7 +242,12 @@ def rank_program(g, core, T, topo):
     if rank != 0:
         act(A("win", 256 + V, 256 + 2 * V), A("win", 256, 256 + V), ACT.Identity, bias=float(R))
     vcopy(A("wf", 0, 1), A("w_s", 0, 1))
-    vts(A("thf", 0, 1), A("th_s", 0, 1), -2048.0, None, ALU.add)
+    vts(A("thf", 0, 1), A("th_s", 0, 1), -1.0, -0.5, ALU.mult, ALU.add)
+    vts(A("thf", 1, 2), A("th_s", 0, 1), -2048.0, None, ALU.add)
+    vts(A("tb", 0, 1), A("di", 0, 1), float(2 ** 17), float(1 - 2 ** 17), ALU.mult, ALU.add)
+    vts(A("tb", 1, 2), A("di", 0, 1), float(2 ** 17), float(1 - 2 ** 17 + 37 * 2048), ALU.mult, ALU.add)
+    vts(M("t18h"), M("tmpa"), float(2 ** 17), None, ALU.mult)
+    vts(M("g20h"), M("gg"), float(2 ** 19), None, ALU.mult)
     vts(M("w16"), M("gg"), A("wf", 0, 1), None, ALU.mult)
 
     def ext(sem, cnt, wr):
@@ -248,15 +256,15 @@ def rank_program(g, core, T, topo):
     n_far = nmask(topo, helper_of(T, topo, (rank - 1) % N), core)
     for k, n_ in ((1, n_far), (2, nmask(topo, T.cores[(rank + 2) % N], core)),
                   (3, nmask(topo, helper_of(T, topo, (rank + 1) % N), core))):
-        ops[ext("a%d" % k, n_, [A("nat", k * L, k * L + L)])]["soft"].append((first[0], 6000))
+        ops[ext("a%d" % k, n_, [A("nat", k * L, k * L + L)])]["soft"].append((first[0], 14000))
 
     def arrivals(t):
         if rank == 0:
             b = (0 - (t + 1)) % N
             src = T.cores[b] if topo.may_write(T.cores[b], core) else helper_of(T, topo, b)
-            ops[ext("m%d_0" % t, nmask(topo, src, core), [A("mi", 32 * t, 32 * t + 16)])]["soft"].append((first[1], 6000))
+            ops[ext("m%d_0" % t, nmask(topo, src, core), [A("mi", 32 * t, 32 * t + 16)])]["soft"].append((first[1], 14000))
         else:
-            for s in range(NS):
+            for s in range(NS + 1):
                 c0, c1 = msg_cols(t, s)
                 ops[ext("m%d_%d" % (t, s), n_far, [A("mi", c0, c1)])]["soft"].append((mark[(t, s)], CFG["hop"]))
 
@@ -281,8 +289,9 @@ def rank_program(g, core, T, topo):
         vcopy(A("key3", 0, 16), koff(0, L))
         vcopy(A("kb", 0, L), IND(A("iow", 0, V), koff(0, L)))
         if not fresh:
-            vts(A("mneg", 0, 16), moff(0, L), 1024.0, -float(2 ** 21), ALU.is_ge, ALU.mult)
-            act(A("mb", 0, L), IND(A("iow", 0, 2 * V), moff(0, L)), ACT.Relu, bias=-float(V - 1))
+            for l0, l1 in ((0, STAGES[-1][0]), STAGES[-1]):
+                vts(A("mneg", l0 // 16, l1 // 16), moff(l0, l1), 1024.0, -float(2 ** 21), ALU.is_ge, ALU.mult)
+                act(A("mb", l0, l1), IND(A("iow", 0, 2 * V), moff(l0, l1)), ACT.Relu, bias=-float(V - 1))
         for e, l0, l1 in CFG["gat"]:
             src = IND(A("rec_s", 0, R), A("coff", l0, l1))
             if e == "v":
@@ -295,21 +304,25 @@ def rank_program(g, core, T, topo):
             b0, b1 = l0 // 16, l1 // 16
             fin = s == NS - 1
             vts(A("dh", l0, l1), pd(s, l0, l1), -2048.0, None, ALU.add)
-            vts(A("fail", l0, l1), A("dh", l0, l1), A("thf", 0, 1), None, ALU.is_gt)
-            if CFG["t1"][s] == "v":
-                vts(A("t1", l0, l1), A("dh", l0, l1), 37.0, float(37 * 2048 + 1), ALU.mult, ALU.add)
+            if CFG["fl"][s] == "v":
+                vts(A("fail", l0, l1), A("dh", l0, l1), A("thf", 1, 2), 0.5, ALU.is_gt, ALU.subtract)
             else:
-                act(A("t1", l0, l1), pd(s, l0, l1), ACT.Identity, bias=1.0, scale=37.0)
+                act(A("fail", l0, l1), pd(s, l0, l1), ACT.Sign, bias=A("thf", 0, 1))
+            if CFG["t1"][s] == "v":
+                vts(A("t1", l0, l1), A("dh", l0, l1), 37.0, A("tb", 1, 2), ALU.mult, ALU.add)
+            else:
+                act(A("t1", l0, l1), pd(s, l0, l1), ACT.Identity, bias=A("tb", 0, 1), scale=37.0)
+            half = "" if CFG["fl"][s] == "v" else "h"
             q = A("pq", 256 + l0, 256 + l1)
             mm(q, M("ident"), A("cq", l0, l1), True, False)
             mm(q, M("w16"), A("dh", l0, l1), False, False)
-            mm(q, M("g20"), A("fail", l0, l1), False, True)
+            mm(q, M("g20" + half), A("fail", l0, l1), False, True)
             z = pd(s, 256 + l0, 256 + l1)
             if fresh:
-                mm(z, M("t18"), A("fail", l0, l1), True, True)
+                mm(z, M("t18" + half), A("fail", l0, l1), True, True)
             else:
                 mm(z, M("ni18"), A("mb", l0, l1), True, False)
-                mm(z, M("t18"), A("fail", l0, l1), False, True)
+                mm(z, M("t18" + half), A("fail", l0, l1), False, True)
             mark[(t, s)] = vscan(A("sq", l0, l1), A("rq", l0, l1), q, 0.0)
             vtt(A("uu", l0, l1), z, A("t1", l0, l1), ALU.min)
             if fresh:
@@ -322,9 +335,8 @@ def rank_program(g, core, T, topo):
                 vts(A("kj", k0, b1), A("ki", k0, b1), V - 1, None, ALU.bitwise_and)
                 if not last:
                     vcopy(A("mo", 32 * t + b0, 32 * t + b1), A("kj", b0, b1))
-                    if not fin:
-                        c0, c1 = msg_cols(t, s)
-                        mark[(t, s)] = send(hlp, T.mi[:, c0:c1], A("mo", c0, c1), "m%d_%d" % (t, s))
+                    c0, c1 = msg_cols(t, s)
+                    mark[(t, s)] = send(hlp, T.mi[:, c0:c1], A("mo", c0, c1), "m%d_%d" % (t, s))
             vts(A("ee", l0, l1), A("uu", l0, l1), 2047, None, ALU.bitwise_and)
             vtt(A("st", l0, l1), IND(TAB, koff(l0, l1)) if fresh else IND(A("win", 256, 256 + 2 * V), moff(l0, l1)),
                 A("ee", l0, l1), ALU.add)
@@ -345,16 +357,19 @@ def rank_program(g, core, T, topo):
             vcopy(A("soff", b0, b1), A("sz", l0 + 15, l1, 16))
             vtt(IND(A("win", 0, 256 + V), A("soff", b0, b1)), A("st", l0, l1), A("tw", l0, l1), ALU.add)
             if fin:
-                mark[(t, s)] = zs
-            if fin and passes:
+                mark[(t, NS)] = zs
+            if passes and (fin or (s == NS - 2 and not last)):
+                m0 = b0 if fin and not last else 0
                 if not fresh:
-                    vtt(A("mk1", 0, 16), A("sz", 15, L, 16), A("mneg", 0, 16), ALU.subtract)
-                vts(A("mk2", 0, 16), A("sz", 15, L, 16) if fresh else A("mk1", 0, 16), 256.0, 1024.0, ALU.is_ge, ALU.mult)
-                vtt(A("mo16" if last else "mof", 0, 16), A("mk2", 0, 16), A("kj", 0, 16), ALU.add)
+                    vtt(A("mk1", m0, b1), A("sz", 16 * m0 + 15, l1, 16), A("mneg", m0, b1), ALU.subtract)
+                vts(A("mk2", m0, b1), A("sz", 16 * m0 + 15, l1, 16) if fresh else A("mk1", m0, b1), 256.0, 1024.0,
+                    ALU.is_ge, ALU.mult)
+                vtt(A("mo16" if last else "mof", m0, b1), A("mk2", m0, b1), A("kj", m0, b1), ALU.add)
                 if not last:
-                    vcopy(A("mo", 32 * t + 16, 32 * t + 32), A("mof", 0, 16))
-                    c0, c1 = msg_cols(t, s)
-                    mark[(t, s)] = send(hlp, T.mi[:, c0:c1], A("mo", c0, c1), "m%d_%d" % (t, s))
+                    vcopy(A("mo", 32 * t + 16 + m0, 32 * t + 16 + b1), A("mof", m0, b1))
+                    if fin:
+                        c0, c1 = msg_cols(t, NS)
+                        mark[(t, NS)] = send(hlp, T.mi[:, c0:c1], A("mo", c0, c1), "m%d_%d" % (t, NS))
 
         for c0, c1 in CFG["abs"]:
             for c in range(c0, c1):
@@ -433,7 +448,7 @@ def rank_program(g, core, T, topo):
             succ[m].append((n, d))
         left[n] = len(o["pre"])
     prio = [0.0] * len(ops)
-    for n in range(len(ops) - 1, -1, -1):
+    for n in list(range(len(ops) - 1, -1, -1)) * 3:
         prio[n] = max([span(ops[n])] + [d + prio[k] for k, d in succ[n]])
         if rank == 0 and ops[n]["sem"] == "remote" and n + 40 < len(ops):
             prio[n] = max(prio[n + 1:n + 40]) + 500

@@ -1,36 +1,54 @@
 from concourse.mybir import AluOpType as ALU, ActivationFunctionType as ACT
 
 N, V, R, L, NT = 4, 1024, 3072, 256, 4
+TB = 2048
+CR = 327680.0
 CFG = {
+    "blocks": [(0, 64), (64, 128), (128, 192), (192, 256)],
     "stages": [(0, 128), (128, 192), (192, 256)],
-    "gat": [(e, 32 * i, 32 * i + 32) for i, e in enumerate("vssvvvsv")],
-    "abs": [(c, c + 1) for c in range(8)],
-    "red": [(0, 64), (64, 128), (128, 192), (192, 256)],
-    "old": [(0, 32), (32, 64), (64, 128), (128, 192), (192, 256)],
-    "hop": 7000.0, "lat": 200.0, "slack": 0.0, "gam": 1.56, "pe": 0.52, "cy": 0.9,
-    "fl": "vsss", "t1": "vsss",
+    "gat": [(32 * i, 32 * i + 32) for i in range(8)],
+    "old": [(0, 64), (64, 128), (128, 192), (192, 256)],
+    "msgs": ["k0", "k1", "k2", "k3m0", "m1m2"],
+    "on_s": "g1 g2 key3 so0 so1 so2 mm0 mm1 mo0 mo1 mo2 mo3 dh3 kb dh0 dh1 dh2 fl1 rr1",
+    "f32": False,
+    "hop": 5500.0, "lat": 270.0, "beta": 20.0, "sc": 3.8, "gam": 1.56, "pe": 0.47, "cy": 0.88, "vfix": 15.0, "sfix": 40.0,
+    "kint": True,
+    "v": "-st2 -tw2 -w2 -mf1 c0 c1 g0 g3 c2 g4 g5 c3 g7 g6 fl0 sk0 sk1 ki0 ki1 e12 e13 e14 e15 sw0 rr0 ch0 e0 e1 e2 e3 e4 e5 e6 e7 "
+         "sk2 st0 tw0 ki2 ch1 sw1 sz0 e8 e9 e10 e11 mu0 st1 w0 sk3 tw1 mf0 sz1 ki3 sz5 sz4 sz3 sz2 mu1 w1 mu2",
+    "s": "key3 dh0 kb dh1 mb0 mb1 a5 bf0 mo0 mo1 a6 dh2 a7 thr0 bf1 fl1 mo2 rr2 rr1 thr1 dh3 so0 fl2 kf0 mk0 mm0 so1 kf1 mo3 so2 "
+         "mk1 mm1 +g1 +g2 +a0 +a1 +a2 +a3 +a4",
 }
-MAXS = 5
+WID = 192
+EW = 272
+LW = 64
+LB = LW + 32
 
 SCRATCH = {}
 for _dt, _bufs in (
-    ("bfloat16", dict(rec_s=R, at_s=L, nat=4 * L, ones=128, ident=128, g1=128, gg=128, lw=128, tmpa=128, tmpb=128, t18=128,
-                      ni18=128, t18h=128, g20h=128, tz=128, g20=128, gn=128, bsel=144, ex=2048, dm=L, cq=L, cz=L, rq=L,
-                      rz=L, xg=16 * L, ab=16 * L, eq=16 * L, mb=L, fail=L)),
-    ("float16", dict(id16=128, w16=128, kb=L, dh=L, mo16=16)),
-    ("int32", dict(ch_s=V, k0_s=16, th_s=4, w_s=4, di=L, d16=16, uu=L, ee=L, ki=16, kj=16)),
+    ("bfloat16", dict(rec_s=R, at_s=L, atb=4 * L, ones=L, ident=128, g1=128, gg=128, gh=128, gn=128, gp=128, gm=128, tz0=128,
+                      tz=128, tzh=128, dg=128, bsel=144, ex=2048, dm=WID, cw=WID, cz=WID, ck2=WID, rw=WID, xg=16 * L, ab=16 * L,
+                      mb=2 * L, fail=L, rr=L)),
+    ("float16", dict(id16=128, id37=128, w16=128, ck=WID, kb=2 * L, dh=L, c16=L, mo16=16)),
+    ("int32", dict(ch_s=V, k0_s=16, th_s=4, w_s=4, di=WID, ki=16, ski=L)),
     ("uint16", dict(k0u=16, mi=96, mo=96, coff=L, soff=16)),
-    ("float32", dict(thf=4, tb=4, wf=4, win=256 + 2 * V, iow=2 * V, key3=16, mneg=16, wantv=16, t1=L, st=L, tw=L, sq=L,
-                     sz=L, mk1=16, mk2=16, mof=16, ykb=L)),
+    ("float32", dict(id32=128, thf=4, col=4, wf=4, win=TB + 2 * V, iow=2 * V, key3=32, thr=32, rk=WID, rz=WID, bf=L, st=L, tw=L,
+                     sw=L, sk=L, sz=L, kf=16, mk=16, mof=16, ykb=L)),
 ):
     for _k, _n in _bufs.items():
         SCRATCH[_k] = ("sbuf", [128, _n], _dt)
-PSUM = dict(py=2048, pd0=512, pd1=512, pq=512, pz=512)
+SCRATCH["eq"] = ("sbuf", [128, 16, EW], "bfloat16")
+SCRATCH["et"] = ("sbuf", [128, 4, LW], "bfloat16")
+SCRATCH["dl"] = ("sbuf", [128, 4, LW], "float32")
+SCRATCH["cl"] = ("sbuf", [128, 4, LB], "bfloat16")
+SCRATCH["rl"] = ("sbuf", [128, 4, LB], "float32")
+SCRATCH["sl"] = ("sbuf", [128, 4, LB], "float32")
+PSUM = dict(py=1536, pd0=512, pd1=512, pq=512, pz=512, pl=512)
 for _k, _n in PSUM.items():
     SCRATCH[_k] = ("psum", [128, _n], "float32")
+SCRATCH["pl"] = ("psum", [128, 4, 128], "float32")
 SEMAPHORES = (["qv", "qs", "qt", "qg", "sent", "a0", "a1", "a2", "a3", "k0"]
-              + ["m%d_%d" % (t, s) for t in range(NT - 1) for s in range(MAXS)]
-              + ["l_at", "l_k0", "l_th", "l_w", "l_ch", "l_c1", "l_r0", "l_r1", "o_c0", "o_c1", "o_k"])
+              + ["%s%d_%d" % (k, s, t) for t in range(NT - 1) for s in range(5) for k in "km"]
+              + ["l_at", "l_k0", "l_th", "l_w", "l_ch", "l_c1", "l_r0", "l_r1", "l_hi", "o_c0", "o_c1", "o_k"])
 
 
 def helper_of(T, topo, r):
@@ -50,12 +68,10 @@ def rsend(g, T, topo, src, dst, out_ap, in_ap, sem):
     return nmask(topo, src, dst)
 
 
-def msg_cols(t, s):
-    st = CFG["stages"]
-    cut = 16 + st[-1][0] // 16
-    if s == len(st):
-        return 32 * t + cut, 32 * t + 32
-    return 32 * t + st[s][0] // 16, 32 * t + (cut if s == len(st) - 1 else st[s][1] // 16)
+def msg_cols(t, m):
+    def col(p, end):
+        return 32 * t + (0 if p[0] == "k" else 16) + CFG["blocks" if p[0] == "k" else "stages"][int(p[1])][end] // 16
+    return col(m[:2], 0), col(m[-2:], 1)
 
 
 def helper_program(g, core, T, topo, r):
@@ -63,19 +79,71 @@ def helper_program(g, core, T, topo, r):
     n_in = nmask(topo, me, core)
     sent = 0
     g.wait_ge(T.sem["a0"], n_in)
-    sent += rsend(g, T, topo, core, T.cores[(r + 1) % N], T.nat[:, L:2 * L], T.nat[:, 0:L], "a1")
+    sent += rsend(g, T, topo, core, T.cores[(r + 1) % N], T.atb[:, L:2 * L], T.atb[:, 0:L], "a1")
     if not topo.may_write(me, T.cores[0]) and r != 0:
         t = (0 - r) % N
         g.wait_ge(T.sem["k0"], n_in)
-        sent += rsend(g, T, topo, core, T.cores[0], T.mi[:, 32 * (t - 1):32 * (t - 1) + 16], T.k0u[:, 0:16], "m%d_0" % (t - 1))
-    sent += rsend(g, T, topo, core, T.cores[(r + 3) % N], T.nat[:, 3 * L:4 * L], T.nat[:, 0:L], "a3")
+        sent += rsend(g, T, topo, core, T.cores[0], T.mi[:, 32 * (t - 1):32 * (t - 1) + 16], T.k0u[:, 0:16], "k0_%d" % (t - 1))
+    sent += rsend(g, T, topo, core, T.cores[(r + 3) % N], T.atb[:, 3 * L:4 * L], T.atb[:, 0:L], "a3")
     if r < N - 1:
         for t in range(NT - 1):
-            for s in range(len(CFG["stages"]) + 1):
-                c0, c1 = msg_cols(t, s)
-                g.wait_ge(T.sem["m%d_%d" % (t, s)], n_in)
-                sent += rsend(g, T, topo, core, T.cores[r + 1], T.mi[:, c0:c1], T.mi[:, c0:c1], "m%d_%d" % (t, s))
+            for m in CFG["msgs"]:
+                c0, c1 = msg_cols(t, m)
+                g.wait_ge(T.sem["%s_%d" % (m[:2], t)], n_in)
+                sent += rsend(g, T, topo, core, T.cores[r + 1], T.mi[:, c0:c1], T.mi[:, c0:c1], "%s_%d" % (m[:2], t))
     g.wait_ge(T.sem["sent"], sent)
+
+
+def arrange(ops, named):
+    span = [o["cost"] if o["done"] is None else o["done"] for o in ops]
+    succ = [[] for _ in ops]
+    left = [0] * len(ops)
+    for n, o in enumerate(ops):
+        for m, d in ([(m, span[m] + CFG["lat"]) for m in o["hard"]] + [(m, ops[m]["cost"]) for m in o["order"]] + o["soft"]):
+            succ[m].append((n, d))
+            left[n] += 1
+    for q in "vs":
+        line = [named.get((t + name.count("+") - name.count("-"), name.strip("+-"))) for t in range(-1, NT + 1)
+                for name in CFG[q].split()]
+        line = [n for n in line if n is not None and ops[n]["q"] == q]
+        for m, n in zip(line, line[1:]):
+            succ[m].append((n, ops[m]["cost"]))
+            left[n] += 1
+    line = [n for n in range(len(ops)) if left[n] == 0]
+    pool = {q: [n for n in line if ops[n]["q"] == q] for q in "vstgyx"}
+    todo = list(left)
+    for n in line:
+        for k, d in succ[n]:
+            todo[k] -= 1
+            if todo[k] == 0:
+                line.append(k)
+    if len(line) < len(ops):
+        return None
+    prio = list(span)
+    for n in line[::-1]:
+        for k, d in succ[n]:
+            prio[n] = max(prio[n], d + prio[k])
+    ready = [0.0] * len(ops)
+    free = {q: 0.0 for q in pool}
+    pick, seq = {}, []
+    while len(seq) < len(ops):
+        for q, c in pool.items():
+            if c and q not in pick:
+                t0 = max(free[q], min(ready[k] for k in c))
+                n = max(c, key=lambda k: (prio[k] - CFG["beta"] * max(0.0, ready[k] - t0), -k))
+                pick[q] = (max(t0, ready[n]), n)
+        q = min(pick, key=pick.get)
+        t1, n = pick.pop(q)
+        pool[q].remove(n)
+        free[q] = t1 + ops[n]["cost"]
+        seq.append(n)
+        for k, d in succ[n]:
+            ready[k] = max(ready[k], t1 + d)
+            left[k] -= 1
+            if left[k] == 0:
+                pool[ops[k]["q"]].append(k)
+                pick.pop(ops[k]["q"], None)
+    return seq
 
 
 def rank_program(g, core, T, topo):
@@ -85,50 +153,53 @@ def rank_program(g, core, T, topo):
             if helper_of(T, topo, r) == core:
                 helper_program(g, core, T, topo, r)
         return
-    STAGES = CFG["stages"]
-    NS = len(STAGES)
+    BLOCKS, STAGES = CFG["blocks"], CFG["stages"]
+    NB, NS = len(BLOCKS), len(STAGES)
     CY, GAM, LAT = CFG["cy"], CFG["gam"], CFG["lat"]
+    ON_S = CFG["on_s"].split()
+    PARTS = [(STAGES[int(m[m.index("m") + 1])][0], STAGES[int(m[-1])][1], m[-2:]) for m in CFG["msgs"] if "m" in m]
     hlp = helper_of(T, topo, rank)
     ops = []
     sent = [0]
-    mark = {}
+    named = {}
+    bank_no = [0]
 
     def A(name, lo, hi, step=1, p1=128):
         ap = T[name][0:p1, lo:hi:step] if step != 1 else T[name][0:p1, lo:hi]
-        return (ap, (name, lo, hi, step))
+        return (ap, [(name, lo, hi, step)], (hi - lo + step - 1) // step)
+
+    def B(name, b0, b1, c0, c1):
+        w = SCRATCH[name][1][2]
+        ap = T[name][:, b0, c0:c1] if b1 == b0 + 1 else T[name][:, b0:b1, c0] if c1 == c0 + 1 else T[name][:, b0:b1, c0:c1]
+        return (ap, [(name, w * b + c0, w * b + c1, 1) for b in range(b0, b1)], (b1 - b0) * (c1 - c0))
 
     def IND(w, o):
-        return (w[0].indirect(o[0]), w[1], o[1])
+        return (w[0].indirect(o[0]), w[1] + o[1], 16 * o[2], w, o)
 
     def regs(xs):
         out = []
         for x in xs:
             if isinstance(x, tuple):
-                out.extend(x[1:])
+                out.extend(x[1])
         return out
 
     def val(x):
         return x[0] if isinstance(x, tuple) else x
 
-    def nel(x):
-        r_ = x[-1]
-        n = (r_[2] - r_[1] + r_[3] - 1) // r_[3]
-        return 16 * n if len(x) == 3 else n
-
     def two(x):
-        return SCRATCH[x[1][0]][2] in ("bfloat16", "float16", "uint16")
+        return SCRATCH[x[1][0][0]][2] in ("bfloat16", "float16", "uint16")
 
     def add(q, fn, rd, wr, cost, sem=None, done=None):
         ops.append({"q": q, "fn": fn, "rd": regs(rd), "wr": regs(wr), "sem": sem, "inc": False, "cost": cost,
-                    "done": done, "soft": []})
+                    "done": done, "soft": [], "name": None})
         return len(ops) - 1
 
     def vcost(o, i, per=None):
-        if len(i) == 3:
-            return 50 + nel(i) * GAM * CY
+        if len(i) > 3:
+            return 50 + i[2] * GAM * CY
         if per is None:
             per = 0.5 if two(o) and two(i) else 1.0
-        return max(64, nel(o) * per) * CY
+        return CFG["vfix"] + max(64, o[2] * per) * CY
 
     def vcopy(o, i):
         return add("v", lambda: g.vector.tensor_copy(o[0], i[0]), [i], [o], vcost(o, i))
@@ -139,10 +210,9 @@ def rank_program(g, core, T, topo):
         return add("v", lambda: g.vector.tensor_scalar(o[0], i[0], val(s1), val(s2), op0, op1), [i, s1, s2], [o], vcost(o, i))
 
     def vtt(o, a, b, op):
-        if len(o) == 3:
-            return add("v", lambda: g.vector.tensor_tensor(o[0], a[0], b[0], op), [a, b, (None, o[2])], [(None, o[1])],
-                       50 + nel(o) * 3.8 * CY)
-        per = 1.0 if a[1][0] in PSUM or b[1][0] in PSUM else 2.0
+        if len(o) > 3:
+            return add("v", lambda: g.vector.tensor_tensor(o[0], a[0], b[0], op), [a, b, o[4]], [o[3]], 50 + o[2] * CFG["sc"] * CY)
+        per = 1.0 if a[1][0][0] in PSUM or b[1][0][0] in PSUM else 2.0
         return add("v", lambda: g.vector.tensor_tensor(o[0], a[0], b[0], op), [a, b], [o], vcost(o, a, per))
 
     def vset(o, c):
@@ -150,17 +220,25 @@ def rank_program(g, core, T, topo):
 
     def vscan(o, d0, d1, init):
         return add("v", lambda: g.vector.tensor_tensor_scan(o[0], d0[0], d1[0], init, ALU.min, ALU.max), [d0, d1], [o],
-                   vcost(o, d1))
+                   vcost(o, d1, 1.0))
 
     def act(o, i, f, bias=None, scale=1.0):
-        cost = 65 + nel(i) * (GAM if len(i) == 3 else 1.0) * CY
+        cost = 65 + i[2] * GAM * CY if len(i) > 3 else CFG["sfix"] + i[2] * CY
         if bias is not None:
             return add("s", lambda: g.scalar.activation(o[0], i[0], f, bias=val(bias), scale=scale), [i, bias], [o], cost)
         return add("s", lambda: g.scalar.activation(o[0], i[0], f), [i], [o], cost)
 
+    def lin(e, o, i, scale=1.0, bias=0.0):
+        if e == "s":
+            return act(o, i, ACT.Identity, bias=bias, scale=scale)
+        return vcopy(o, i) if (scale, bias) == (1.0, 0.0) else vts(o, i, scale, bias, ALU.mult, ALU.add)
+
     def mm(o, lh, rh, start, stop):
         return add("t", lambda: g.tensor.matmul(o[0], lh[0], rh[0], start, stop), [lh, rh], [o],
-                   max(min(64, nel(lh)), nel(rh)) * CFG["pe"])
+                   max(min(64, lh[2]), rh[2]) * CFG["pe"] * (1 if two(lh) else 4))
+
+    def group(terms):
+        return [mm(o, lh, rh, n == 0, n == len(terms) - 1) for n, (o, lh, rh) in enumerate(terms)]
 
     def dma(q, o, i, sem, done):
         eng = g.sync if q == "y" else g.scalar
@@ -175,79 +253,93 @@ def rank_program(g, core, T, topo):
 
     dma("y", A("at_s", 0, L), T.at[:], "l_at", 2200)
     dma("s", A("k0_s", 0, 16), T.key0[:], "l_k0", 2300)
-    dma("y", A("ch_s", 0, V // 2), T.ch[:, 0:V // 2], "l_ch", 4300)
-    dma("s", A("ch_s", V // 2, V), T.ch[:, V // 2:V], "l_c1", 4300)
-    dma("y", A("rec_s", 0, R // 2), T.rec[:, 0:R // 2], "l_r0", 7300)
-    dma("s", A("rec_s", R // 2, R), T.rec[:, R // 2:R], "l_r1", 7300)
-    dma("y", A("th_s", 0, 1), T.th[:], "l_th", 8000)
-    dma("s", A("w_s", 0, 1), T.w[:], "l_w", 8000)
+    dma("y", A("ch_s", 0, V // 2), T.ch[:, 0:V // 2], "l_ch", 3800)
+    dma("s", A("ch_s", V // 2, V), T.ch[:, V // 2:V], "l_c1", 3800)
+    dma("y", A("rec_s", 0, R // 2), T.rec[:, 0:R // 2], "l_r0", 6000)
+    dma("s", A("rec_s", R // 2, R), T.rec[:, R // 2:R], "l_r1", 6000)
+    dma("y", A("th_s", 0, 1), T.th[:], "l_th", 6500)
+    dma("s", A("w_s", 0, 1), T.w[:], "l_w", 6500)
     n_loads = len(ops)
 
-    def sel(o, i, pat, op, base, cm):
-        add("g", lambda: g.affine_select(o[0], i[0], pat, op, 0.0, base, cm), [i], [o], 210 + 2 * CY * nel(o))
+    def sel(o, i, pat, op, base, cm, fill=0.0):
+        add("g", lambda: g.affine_select(o[0], i[0], pat, op, fill, base, cm), [i], [o], 170 + 2 * CY * o[2])
 
     def iota(o, pat, base, cm, small=False):
         if small:
-            add("g", lambda: g.iota(o[0], pat, base, cm, allow_small_or_imprecise_dtypes=True), [], [o], 160 + 2 * CY * nel(o))
+            add("g", lambda: g.iota(o[0], pat, base, cm, allow_small_or_imprecise_dtypes=True), [], [o], 130 + 2 * CY * o[2])
         else:
-            add("g", lambda: g.iota(o[0], pat, base, cm), [], [o], 160 + 2 * CY * nel(o))
+            add("g", lambda: g.iota(o[0], pat, base, cm), [], [o], 130 + 2 * CY * o[2])
 
-    vset(M("ones"), 1.0)
+    W = max(l1 - l0 for l0, l1 in STAGES + BLOCKS)
+    lw = STAGES[-1][1] - STAGES[-1][0]
+    nl = lw // 16
+    vset(A("ones", 0, L), 1.0)
     sel(M("ident"), M("ones"), [[-1, 128]], ALU.is_equal, 0, 1)
     sel(M("g1"), M("ones"), [[-16, 8], [0, 16]], ALU.is_ge, 0, 1)
     sel(M("gg"), M("g1"), [[16, 8], [0, 16]], ALU.is_ge, 15, -1)
-    iota(A("di", 0, L), [[0, 16], [-1, 16]], 16, 1)
-    sel(M("lw"), M("gg"), [[1, 128]], ALU.is_gt, 0, -1)
-    iota(A("d16", 0, 16), [[1, 16]], 0, 16)
-    vset(A("iow", V, 2 * V), 2047.0)
-    vset(A("win", 0, 256), 0.0)
+    iota(A("di", 0, W), [[0, W // 16], [-1, 16]], 16, 1)
+    lin("s", M("gn"), M("gg"), -8192.0)
+    sel(M("tz0"), M("gn"), [[1, 128]], ALU.is_gt, 0, -1)
+    sel(M("tz"), M("tz0"), [[1, 128]], ALU.not_equal, 0, -1, 4096.0)
     vset(A("bsel", 0, 144), 0.0)
-    vset(A("rq", 0, L), float(2 ** 27))
-    vset(A("rz", 0, L), 4096.0)
-    vset(A("rq", 0, L, 16), -float(2 ** 27))
+    vset(A("rz", 0, W), 4096.0)
+    iota(A("rz", 0, W, 16), [[-1, W // 16]], 15, 16, True)
+    vset(A("rw", 0, W), 4096.0)
+    vset(A("rw", 0, W, 16), 0.0)
+    big = float(2 ** 22) if CFG["kint"] else 4096.0
+    vset(A("rk", 0, W), big)
+    vset(A("rk", 0, W, 16), -big)
+    vset(B("rl", 0, nl, 0, LB), -4096.0)
+    iota(B("rl", 0, nl, LB - 1, LB), [[1, nl]], 0, 16, True)
+    iota(B("dl", 0, nl, 0, LW), [[16, nl], [-1, LW]], 0, 0, True)
+    iota(A("iow", 0, V), [[1, V]], 0, 0, True)
     for h in range(2):
         mm(A("pq", 128 * h, 128 * h + 128), A("at_s", 128 * h, 128 * h + 128), M("ident"), True, True)
     for i in range(16):
-        if i % 2 == 0:
-            act(A("ex", i, 2048, 16), M("ident"), ACT.Copy)
-        else:
-            vcopy(A("ex", i, 2048, 16), M("ident"))
-    vts(A("nat", 0, L), A("pq", 0, L), -1.0, None, ALU.mult)
+        lin("sv"[i % 2], A("ex", i, 2048, 16), M("ident"))
+    lin("s", A("atb", 0, L), A("pq", 0, L), -1.0)
     vcopy(A("k0u", 0, 16), A("k0_s", 0, 16))
-    first = [send(hlp, T.nat[:, 0:L], A("nat", 0, L), "a0")]
+    first = [send(hlp, T.atb[:, 0:L], A("atb", 0, L), "a0")]
     if rank != 0:
         t = (0 - rank) % N
         if topo.may_write(core, T.cores[0]):
-            first.append(send(T.cores[0], T.mi[:, 32 * (t - 1):32 * (t - 1) + 16], A("k0u", 0, 16), "m%d_0" % (t - 1)))
+            first.append(send(T.cores[0], T.mi[:, 32 * (t - 1):32 * (t - 1) + 16], A("k0u", 0, 16), "k0_%d" % (t - 1)))
         else:
             first.append(send(hlp, T.k0u[:, 0:16], A("k0u", 0, 16), "k0"))
-    first.append(send(T.cores[(rank + 2) % N], T.nat[:, 2 * L:3 * L], A("nat", 0, L), "a2"))
-    iota(A("iow", 0, V), [[1, V]], 0, 0, True)
-    vcopy(A("bsel", 15, 128, 16), A("gg", 0, 128, 16))
-    vts(A("di", 0, L), A("di", 0, L), 15, None, ALU.bitwise_and)
-    vts(A("d16", 0, 16), A("d16", 0, 16), 255, None, ALU.bitwise_and)
-    vtt(M("tmpa"), M("ident"), M("lw"), ALU.subtract)
-    vts(A("dm", 0, L), A("di", 0, L), 0.0, None, ALU.is_equal)
-    vts(A("rz", 0, L, 16), A("d16", 0, 16), -1.0, 255.0, ALU.mult, ALU.add)
-    vtt(M("tmpb"), M("tmpa"), M("lw"), ALU.subtract)
-    vts(M("t18"), M("tmpa"), float(2 ** 18), None, ALU.mult)
-    vts(A("cq", 0, L), A("dm", 0, L), float(2 ** 26 + 15 * 2 ** 19), -float(2 ** 26), ALU.mult, ALU.add)
-    vts(A("cz", 0, L), A("dm", 0, L), 8192.0 - 1792.0, -8192.0, ALU.mult, ALU.add)
-    vts(M("tz"), M("tmpb"), 2048.0, None, ALU.mult)
-    vts(M("ni18"), M("ident"), -float(2 ** 18), None, ALU.mult)
-    vts(M("g20"), M("gg"), float(2 ** 20), None, ALU.mult)
-    vts(M("gn"), M("gg"), -4096.0, None, ALU.mult)
-    vcopy(M("id16"), M("ident"))
-    vcopy(A("win", 256, 256 + V), A("ch_s", 0, V))
+    first.append(send(T.cores[(rank + 2) % N], T.atb[:, 2 * L:3 * L], A("atb", 0, L), "a2"))
     if rank != 0:
-        act(A("win", 256 + V, 256 + 2 * V), A("win", 256, 256 + V), ACT.Identity, bias=float(R))
-    vcopy(A("wf", 0, 1), A("w_s", 0, 1))
-    vts(A("thf", 0, 1), A("th_s", 0, 1), -1.0, -0.5, ALU.mult, ALU.add)
-    vts(A("thf", 1, 2), A("th_s", 0, 1), -2048.0, None, ALU.add)
-    vts(A("tb", 0, 1), A("di", 0, 1), float(2 ** 17), float(1 - 2 ** 17), ALU.mult, ALU.add)
-    vts(A("tb", 1, 2), A("di", 0, 1), float(2 ** 17), float(1 - 2 ** 17 + 37 * 2048), ALU.mult, ALU.add)
-    vts(M("t18h"), M("tmpa"), float(2 ** 17), None, ALU.mult)
-    vts(M("g20h"), M("gg"), float(2 ** 19), None, ALU.mult)
+        iota(A("iow", V, 2 * V), [[0, V]], V, 0, True)
+    vcopy(A("bsel", 15, 128, 16), A("gg", 0, 128, 16))
+    vts(A("di", 0, W), A("di", 0, W), 15, None, ALU.bitwise_and)
+    vts(A("dm", 0, W), A("di", 0, W), 0.0, None, ALU.is_equal)
+    lin("s", A("cw", 0, W), A("dm", 0, W), 2048.0 + 8.0, -2048.0)
+    if CFG["kint"]:
+        lin("s", A("ck2", 0, W), A("dm", 0, W), float(2 ** 21 + 2 ** 19), -float(2 ** 21))
+    else:
+        lin("s", A("ck", 0, W), A("dm", 0, W), 2048.0 - 1023.0 / 2048, -2048.0)
+    lin("s", A("cz", 0, W), A("dm", 0, W), 16384.0 + TB - 4096.0, -16384.0)
+    lin("s", M("id16"), M("ident"))
+    lin("s", M("id37"), M("ident"), 37.0)
+    lin("s", M("gp"), M("gg"), 4096.0)
+    lin("s", M("gm"), M("gg"), -4096.0)
+    lin("s", M("tzh"), M("tz"), 0.5)
+    lin("s", M("gh"), M("gg"), 0.5)
+    lin("v", A("col", 0, 1), A("di", 0, 1))
+    lin("v", A("col", 1, 2), A("di", 0, 1), -4096.0, 37 * 2048 + CR - (2048 if CFG["f32"] else 0))
+    if CFG["f32"]:
+        lin("s", M("id32"), M("ident"))
+    vts(M("dg"), M("ident"), A("col", 1, 2), None, ALU.mult)
+    vts(B("dl", 0, nl, 0, LW), B("dl", 0, nl, 0, LW), A("col", 0, 1), 0.0, ALU.add, ALU.is_le)
+    lin("s", B("cl", 0, nl, 32, LB), B("dl", 0, nl, 0, LW), float(2 ** 19), float(2 ** 18 + 4096 - 65536))
+    lin("s", B("cl", 0, nl, 0, 16), A("dm", 0, lw), -float(2 ** 19), float(2 ** 19 + 61440))
+    lin("s", B("cl", 0, nl, 16, 32), A("dm", 0, lw), float(TB - 2 ** 22), float(2 ** 22))
+    vcopy(A("win", TB, TB + V), A("ch_s", 0, V))
+    if rank != 0:
+        dma("y", A("win", TB + V, TB + 2 * V), A("win", TB, TB + V), "l_hi", 4000)
+    lin("v", A("wf", 0, 1), A("w_s", 0, 1), 1.0 if CFG["kint"] else 1.0 / V)
+    lin("v", A("thf", 0, 1), A("th_s", 0, 1), -1.0, -0.5)
+    lin("v", A("thf", 1, 2), A("th_s", 0, 1), 1.0, -2048.0)
+    lin("v", A("thf", 2, 3), A("th_s", 0, 1), -1.0, 2047.5)
     vts(M("w16"), M("gg"), A("wf", 0, 1), None, ALU.mult)
 
     def ext(sem, cnt, wr):
@@ -256,24 +348,39 @@ def rank_program(g, core, T, topo):
     n_far = nmask(topo, helper_of(T, topo, (rank - 1) % N), core)
     for k, n_ in ((1, n_far), (2, nmask(topo, T.cores[(rank + 2) % N], core)),
                   (3, nmask(topo, helper_of(T, topo, (rank + 1) % N), core))):
-        ops[ext("a%d" % k, n_, [A("nat", k * L, k * L + L)])]["soft"].append((first[0], 14000))
+        ops[ext("a%d" % k, n_, [A("atb", k * L, k * L + L)])]["soft"].append((first[0], 8000))
+
+    def twin(t, m):
+        m = [x for x in CFG["msgs"] if m in x][0]
+        return named.get((t, "send " + m), named.get((t, ("dh" if m[-2] == "k" else "so") + m[-1])))
 
     def arrivals(t):
         if rank == 0:
             b = (0 - (t + 1)) % N
             src = T.cores[b] if topo.may_write(T.cores[b], core) else helper_of(T, topo, b)
-            ops[ext("m%d_0" % t, nmask(topo, src, core), [A("mi", 32 * t, 32 * t + 16)])]["soft"].append((first[1], 14000))
+            ops[ext("k0_%d" % t, nmask(topo, src, core), [A("mi", 32 * t, 32 * t + 16)])]["soft"].append((first[1], 8000))
         else:
-            for s in range(NS + 1):
-                c0, c1 = msg_cols(t, s)
-                ops[ext("m%d_%d" % (t, s), n_far, [A("mi", c0, c1)])]["soft"].append((mark[(t, s)], CFG["hop"]))
+            for m in CFG["msgs"]:
+                c0, c1 = msg_cols(t, m)
+                n = ext("%s_%d" % (m[:2], t), n_far, [A("mi", c0, c1)])
+                ops[n]["soft"].append((twin(t, m), CFG["hop"] + (0 if rank < N - 1 else 1500)))
+                ops[n]["name"] = (t, "take " + m)
 
-    TAB = A("win", 256, 256 + V)
+    TAB = A("win", TB, TB + V)
 
     def one_round(t):
         fresh = t == 0 or rank == 0
         last = t == NT - 1
         passes = last or rank < N - 1
+        sends = []
+
+        def nm(name, n):
+            ops[n]["name"] = (t, name)
+            named[(t, name)] = n
+            return n
+
+        def on(name):
+            return "s" if name in ON_S else "v"
 
         def koff(l0, l1):
             return A("k0u", l0 // 16, l1 // 16) if t == 0 else A("mi", 32 * (t - 1) + l0 // 16, 32 * (t - 1) + l1 // 16)
@@ -281,118 +388,154 @@ def rank_program(g, core, T, topo):
         def moff(l0, l1):
             return A("mi", 32 * (t - 1) + 16 + l0 // 16, 32 * (t - 1) + 16 + l1 // 16)
 
-        def pd(s, l0, l1):
-            return A("pd%d" % ((NS * t + s) % 2), l0, l1)
+        def pd(k, l0, l1):
+            return A("pd%d" % ((NB * t + k) % 2), l0, l1)
 
-        for l0, l1 in CFG["old"]:
-            vcopy(A("coff", l0, l1), IND(A("ch_s", 0, V) if t == 0 else TAB, koff(l0, l1)))
-        vcopy(A("key3", 0, 16), koff(0, L))
-        vcopy(A("kb", 0, L), IND(A("iow", 0, V), koff(0, L)))
-        if not fresh:
-            for l0, l1 in ((0, STAGES[-1][0]), STAGES[-1]):
-                vts(A("mneg", l0 // 16, l1 // 16), moff(l0, l1), 1024.0, -float(2 ** 21), ALU.is_ge, ALU.mult)
-                act(A("mb", l0, l1), IND(A("iow", 0, 2 * V), moff(l0, l1)), ACT.Relu, bias=-float(V - 1))
-        for e, l0, l1 in CFG["gat"]:
-            src = IND(A("rec_s", 0, R), A("coff", l0, l1))
-            if e == "v":
-                vcopy(A("xg", 16 * l0, 16 * l1), src)
+        def P(name, l0, l1):
+            w = SCRATCH[name][1][1] // 2
+            return A(name, w * (t % 2) + l0, w * (t % 2) + l1)
+
+        def as_if(n, m):
+            if rank == 0 and t > 0:
+                ops[n]["soft"].append((twin(t - 1, m), CFG["hop"]))
+
+        for n, (l0, l1) in enumerate(CFG["old"]):
+            as_if(nm("c%d" % n, lin(on("c%d" % n), A("coff", l0, l1), IND(A("ch_s", 0, V) if t == 0 else TAB, koff(l0, l1)))),
+                  "k%d" % [k for k in range(NB) if BLOCKS[k][0] < l1][-1])
+        nm("key3", lin(on("key3"), P("key3", 0, 16), koff(0, L)))
+        nm("kb", lin(on("kb"), P("kb", 0, L), IND(A("iow", 0, V), koff(0, L))))
+        for s, (l0, l1, m) in enumerate(PARTS):
+            if not CFG["f32"]:
+                nm("ch%d" % s, lin(on("ch%d" % s), A("c16", l0, l1), A("coff", l0, l1), 1.0, -2047.0))
+            if fresh:
+                as_if(nm("bf%d" % s, lin("s", A("bf", l0, l1), A("coff", l0, l1))), m)
             else:
-                act(A("xg", 16 * l0, 16 * l1), src, ACT.Copy)
+                nm("bf%d" % s, lin("s", A("bf", l0, l1), IND(A("win", TB, TB + 2 * V), moff(l0, l1))))
+                if passes:
+                    nm("thr%d" % s, act(P("thr", l0 // 16, l1 // 16), moff(l0, l1), ACT.Relu, bias=-4096.0 * (V - 1), scale=4096.0))
+                nm("mb%d" % s, act(P("mb", l0, l1), IND(A("iow", 0, 2 * V), moff(l0, l1)), ACT.Relu, bias=-float(V - 1)))
+        for n, (l0, l1) in enumerate(CFG["gat"]):
+            nm("g%d" % n, lin(on("g%d" % n), A("xg", 16 * l0, 16 * l1), IND(A("rec_s", 0, R), A("coff", l0, l1))))
+
+        def block(k):
+            l0, l1 = BLOCKS[k]
+            b0, b1 = l0 // 16, l1 // 16
+            if k == NB - 1:
+                nm("fl%d" % (NS - 1), act(A("fail", l0, l1), pd(k, l0, l1), ACT.Sign, bias=A("thf", 0, 1)))
+                nm("rr%d" % (NS - 1), lin("s", A("rr", l0, l1), pd(k, l0, l1), -37.0, -(1 - 1023.5 + CR)))
+            nm("dh%d" % k, lin(on("dh%d" % k), A("dh", l0, l1), pd(k, l0, l1), 1.0, -2048.0))
+            if passes:
+                q = pd(k, 256 + l0, 256 + l1)
+                mo = A("mo", 32 * (t % 3) + b0, 32 * (t % 3) + b1)
+                group([(q, M("ident"), A("ck2", 0, l1 - l0)), (q, M("w16"), A("dh", l0, l1))])
+                nm("sk%d" % k, vscan(A("ski", l0, l1), A("rk", 0, l1 - l0), q, 0.0))
+                nm("ki%d" % k, vts(A("ki", b0, b1), A("ski", l0 + 15, l1, 16), V - 1, None, ALU.bitwise_and))
+                if not last:
+                    nm("mo%d" % k, lin(on("mo%d" % k), mo, A("ki", b0, b1)))
 
         def stage(s):
             l0, l1 = STAGES[s]
             b0, b1 = l0 // 16, l1 // 16
             fin = s == NS - 1
-            vts(A("dh", l0, l1), pd(s, l0, l1), -2048.0, None, ALU.add)
-            if CFG["fl"][s] == "v":
-                vts(A("fail", l0, l1), A("dh", l0, l1), A("thf", 1, 2), 0.5, ALU.is_gt, ALU.subtract)
-            else:
-                act(A("fail", l0, l1), pd(s, l0, l1), ACT.Sign, bias=A("thf", 0, 1))
-            if CFG["t1"][s] == "v":
-                vts(A("t1", l0, l1), A("dh", l0, l1), 37.0, A("tb", 1, 2), ALU.mult, ALU.add)
-            else:
-                act(A("t1", l0, l1), pd(s, l0, l1), ACT.Identity, bias=A("tb", 0, 1), scale=37.0)
-            half = "" if CFG["fl"][s] == "v" else "h"
+            marked = [] if fresh else [P("mb", l0, l1)]
+            fl, rr = "fl%d" % s, "rr%d" % s
+            half = fin or on(fl) == "s"
+            if not fin:
+                if half:
+                    nm(fl, act(A("fail", l0, l1), A("dh", l0, l1), ACT.Sign, bias=A("thf", 2, 3)))
+                else:
+                    nm(fl, vts(A("fail", l0, l1), A("dh", l0, l1), A("thf", 1, 2), 0.5, ALU.is_gt, ALU.subtract))
+                nm(rr, lin(on(rr), A("rr", l0, l1), A("dh", l0, l1), -37.0, -(37 * 2048 + 1 - 1023.5 + CR)))
+                q = A("pq", l0, l1)
+                group([(q, M("ident"), A("cw", 0, l1 - l0))] + [(q, M("ident"), m) for m in marked]
+                      + [(q, M("gh" if half else "gg"), A("fail", l0, l1))])
+                nm("sw%d" % s, vscan(A("sw", l0, l1), A("rw", 0, l1 - l0), q, 0.0))
             q = A("pq", 256 + l0, 256 + l1)
-            mm(q, M("ident"), A("cq", l0, l1), True, False)
-            mm(q, M("w16"), A("dh", l0, l1), False, False)
-            mm(q, M("g20" + half), A("fail", l0, l1), False, True)
-            z = pd(s, 256 + l0, 256 + l1)
-            if fresh:
-                mm(z, M("t18" + half), A("fail", l0, l1), True, True)
+            base = ([(q, M("ident"), A("ones", l0, l1)), (q, M("id32"), A("bf", l0, l1))] if CFG["f32"]
+                    else [(q, M("id16"), A("c16", l0, l1))])
+            group([(q, M("dg"), A("ones", l0, l1))] + base + [(q, M("gn"), m) for m in marked]
+                  + [(q, M("id37"), A("dh", l0, l1)), (q, M("tzh" if half else "tz"), A("fail", l0, l1)),
+                     (q, M("ident"), A("rr", l0, l1))])
+            nm("st%d" % s, vtt(A("st", l0, l1), q, A("bf", l0, l1), ALU.max))
+            if on("tw%d" % s) == "v":
+                nm("tw%d" % s, vts(A("tw", l0, l1), q, float(R), -float(R), ALU.is_ge, ALU.mult))
             else:
-                mm(z, M("ni18"), A("mb", l0, l1), True, False)
-                mm(z, M("t18" + half), A("fail", l0, l1), False, True)
-            mark[(t, s)] = vscan(A("sq", l0, l1), A("rq", l0, l1), q, 0.0)
-            vtt(A("uu", l0, l1), z, A("t1", l0, l1), ALU.min)
-            if fresh:
-                vts(A("wantv", b0, b1), A("sq", l0 + 15, l1, 16), 0.0, None, ALU.is_gt)
+                nm("ts%d" % s, act(A("tw", l0, l1), A("st", l0, l1), ACT.Sign, bias=0.5 - R))
+                nm("tw%d" % s, lin("s", A("tw", l0, l1), A("tw", l0, l1), -R / 2, -R / 2))
+            if not fin:
+                z = A("pz", l0, l1)
+                for b in range(b0, b1):
+                    nm("e%d" % b, vts(B("eq", b, b + 1, 0, L - 16 * b), P("kb", 16 * b, L), P("key3", b, b + 1),
+                                      A("sw", 16 * b + 15, 16 * b + 16), ALU.is_equal, ALU.min))
+                group([(z, M("ident"), A("cz", 0, l1 - l0)), (z, M("id16"), P("kb", l0, l1))]
+                      + [(z, M("gn"), B("eq", b, b + 1, l0 - 16 * b, l1 - 16 * b)) for b in range(b0)]
+                      + [(A("pz", 16 * b + 16, l1), M("gn"), B("eq", b, b + 1, 16, l1 - 16 * b)) for b in range(b0, b1 - 1)]
+                      + [(z, M("tz"), B("eq", b0, b1, 0, 16))])
+                nm("sz%d" % s, vscan(A("sz", l0, l1), A("rz", 0, l1 - l0), z, 4096.0))
+                sz = A("sz", l0 + 15, l1, 16)
             else:
-                vtt(A("wantv", b0, b1), A("sq", l0 + 15, l1, 16), A("mneg", b0, b1), ALU.is_gt)
-            if passes and (fin or not last):
-                k0 = 0 if last else b0
-                vcopy(A("ki", k0, b1), A("sq", 16 * k0 + 15, l1, 16))
-                vts(A("kj", k0, b1), A("ki", k0, b1), V - 1, None, ALU.bitwise_and)
-                if not last:
-                    vcopy(A("mo", 32 * t + b0, 32 * t + b1), A("kj", b0, b1))
-                    c0, c1 = msg_cols(t, s)
-                    mark[(t, s)] = send(hlp, T.mi[:, c0:c1], A("mo", c0, c1), "m%d_%d" % (t, s))
-            vts(A("ee", l0, l1), A("uu", l0, l1), 2047, None, ALU.bitwise_and)
-            vtt(A("st", l0, l1), IND(TAB, koff(l0, l1)) if fresh else IND(A("win", 256, 256 + 2 * V), moff(l0, l1)),
-                A("ee", l0, l1), ALU.add)
-            vts(A("tw", l0, l1), A("st", l0, l1), float(R), -float(R), ALU.is_ge, ALU.mult)
-            z = A("pz", l0, l1)
-            mm(z, M("ident"), A("cz", l0, l1), True, False)
-            mm(z, M("id16"), A("kb", l0, l1), False, False)
-            for b in range(b0):
-                mm(z, M("gn"), A("eq", L * b + l0, L * b + l1), False, False)
-            for b in range(b0, b1):
-                vts(A("eq", L * b + 16 * b, L * b + L), A("kb", 16 * b, L), A("key3", b, b + 1), A("wantv", b, b + 1),
-                    ALU.is_equal, ALU.mult)
-                e = 16 * b + 16
-                mm(A("pz", 16 * b, e), M("tz"), A("eq", L * b + 16 * b, L * b + e), False, e == l1)
-                if e < l1:
-                    mm(A("pz", e, l1), M("gn"), A("eq", L * b + e, L * b + l1), False, False)
-            zs = vscan(A("sz", l0, l1), A("rz", l0, l1), z, 4096.0)
-            vcopy(A("soff", b0, b1), A("sz", l0 + 15, l1, 16))
-            vtt(IND(A("win", 0, 256 + V), A("soff", b0, b1)), A("st", l0, l1), A("tw", l0, l1), ALU.add)
-            if fin:
-                mark[(t, NS)] = zs
-            if passes and (fin or (s == NS - 2 and not last)):
-                m0 = b0 if fin and not last else 0
-                if not fresh:
-                    vtt(A("mk1", m0, b1), A("sz", 16 * m0 + 15, l1, 16), A("mneg", m0, b1), ALU.subtract)
-                vts(A("mk2", m0, b1), A("sz", 16 * m0 + 15, l1, 16) if fresh else A("mk1", m0, b1), 256.0, 1024.0,
-                    ALU.is_ge, ALU.mult)
-                vtt(A("mo16" if last else "mof", m0, b1), A("mk2", m0, b1), A("kj", m0, b1), ALU.add)
-                if not last:
-                    vcopy(A("mo", 32 * t + 16 + m0, 32 * t + 16 + b1), A("mof", m0, b1))
-                    if fin:
-                        c0, c1 = msg_cols(t, NS)
-                        mark[(t, NS)] = send(hlp, T.mi[:, c0:c1], A("mo", c0, c1), "m%d_%d" % (t, NS))
+                for b in range(nl):
+                    nm("e%d" % (b0 + b), vts(B("et", b, b + 1, 0, lw), P("kb", l0, l1), P("key3", b0 + b, b0 + b + 1),
+                                             -float(2 ** 18), ALU.is_equal, ALU.mult))
+                own, key = B("pl", 0, nl, 0, 16), B("pl", 0, nl, 16, 32)
+                terms = [(B("pl", 0, nl, 0, LB), M("ident"), B("cl", 0, nl, 0, LB)), (key, M("id16"), P("kb", l0, l1)),
+                         (B("pl", 0, nl, 32, 32 + lw), M("ident"), B("et", 0, nl, 0, lw))]
+                for x in marked + [None, A("fail", l0, l1)]:
+                    if x is None:
+                        terms += [(key, M("gn"), B("eq", b, b + 1, l0 - 16 * b, l1 - 16 * b)) for b in range(b0)]
+                    else:
+                        terms += [(B("pl", b, b + 1, 32, 32 + lw), M("gm"), x) for b in range(nl)] + [(own, M("gp"), x)]
+                group(terms)
+                for b in range(nl):
+                    n = 48 + 16 * b
+                    nm("sz%d" % (s + nl - 1 - b), vscan(B("sl", b, b + 1, LB - n, LB), B("pl", b, b + 1, 0, n),
+                                                        B("rl", b, b + 1, LB - n, LB), 4096.0))
+                sz = B("sl", 0, nl, LB - 1, LB)
+            nm("so%d" % s, lin(on("so%d" % s), A("soff", b0, b1), sz))
+            nm("w%d" % s, vtt(IND(A("win", 0, TB + V), A("soff", b0, b1)), A("st", l0, l1), A("tw", l0, l1), ALU.add))
+            if passes and not fresh:
+                nm("mu%d" % s, vtt(A("mk", b0, b1), sz, P("thr", b0, b1), ALU.add))
 
-        for c0, c1 in CFG["abs"]:
-            for c in range(c0, c1):
-                o = A("py", 512 * (c % 4), 512 * (c % 4) + 512)
-                h = c // 4
-                mm(o, A("nat", L * t + 128 * h, L * t + 128 * h + 128), A("ex", 512 * (c % 4), 512 * (c % 4) + 512), True, False)
-                mm(o, M("ident"), A("xg", 512 * c, 512 * c + 512), False, True)
-            act(A("ab", 512 * c0, 512 * c1), A("py", 512 * (c0 % 4), 512 * (c0 % 4) + 512 * (c1 - c0)), ACT.Abs)
-            for l0, l1 in CFG["red"]:
-                if 32 * c0 < l1 <= 32 * c1:
-                    s = [k for k in range(NS) if STAGES[k][0] <= l0 < STAGES[k][1]][0]
-                    for i in range(16):
-                        mm(pd(s, l0, l1), A("bsel", 15 - i, 15 - i + 128), A("ab", 16 * l0 + i, 16 * l1, 16), i == 0, i == 15)
-                    if l1 == STAGES[s][1]:
-                        stage(s)
+        def marks(s, l0, l1):
+            b0, b1 = l0 // 16, l1 // 16
+            nm("kf%d" % s, lin("s", A("kf", b0, b1), A("ki", b0, b1), 1.0 / 512))
+            nm("mk%d" % s, act(A("mk", b0, b1), A("soff" if fresh else "mk", b0, b1), ACT.Sign, bias=0.5 - TB))
+            nm("mf%d" % s, vtt(A("mof", b0, b1), A("mk", b0, b1), A("kf", b0, b1), ALU.add))
+            nm("mm%d" % s, lin(on("mm%d" % s), A("mo16", b0, b1) if last else A("mo", 32 * t + 16 + b0, 32 * t + 16 + b1),
+                               A("mof", b0, b1), 512.0, 512.0))
+
+        for k, (l0, l1) in enumerate(BLOCKS):
+            for n, (c0, c1) in enumerate(CFG["gat"]):
+                if l0 <= c0 < l1:
+                    y0 = 512 * (bank_no[0] % 3)
+                    bank_no[0] += 1
+                    o = A("py", y0, y0 + 16 * (c1 - c0))
+                    y = group([(o, A("atb", L * t + 128 * (c0 // 128), L * t + 128 * (c0 // 128) + 128),
+                                A("ex", 16 * (c0 % 128), 16 * (c0 % 128 + c1 - c0))),
+                               (o, M("ident"), A("xg", 16 * c0, 16 * c1))])
+                    if t > 0 and n < 3:
+                        ops[y[0]]["soft"].append((named[(t - 1, "sz%d" % (NS - 1))], 0.0))
+                    nm("a%d" % n, act(A("ab", 16 * c0, 16 * c1), o, ACT.Abs))
+            group([(pd(k, l0, l1), A("bsel", 15 - i, 143 - i), A("ab", 16 * l0 + i, 16 * l1, 16)) for i in range(16)])
+            block(k)
+            for s in range(NS):
+                if STAGES[s][1] == l1:
+                    stage(s)
+        if passes:
+            for s, (l0, l1, m) in enumerate([(0, L, "")] if last else PARTS):
+                marks(len(PARTS) - 1 if last else s, l0, l1)
         if not last:
+            if passes:
+                for m in CFG["msgs"]:
+                    c0, c1 = msg_cols(t, m)
+                    nm("send " + m, send(hlp, T.mi[:, c0:c1], A("mo", c0, c1), "%s_%d" % (m[:2], t)))
             arrivals(t)
 
     for t in range(NT):
         one_round(t)
 
-    dma("y", T.yc[:, 0:V // 2], A("win", 256, 256 + V // 2), "o_c0", 3500)
-    dma("s", T.yc[:, V // 2:V], A("win", 256 + V // 2, 256 + V), "o_c1", 3500)
+    dma("y", T.yc[:, 0:V // 2], A("win", TB, TB + V // 2), "o_c0", 3500)
+    dma("s", T.yc[:, V // 2:V], A("win", TB + V // 2, TB + V), "o_c1", 3500)
     for a in range(16):
         mm(A("pq", a, L, 16, 8), A("id16", a, 128, 16), A("mo16", 0, 16), True, True)
     vcopy(A("ykb", 0, L, 1, 8), A("pq", 0, L, 1, 8))
@@ -436,48 +579,9 @@ def rank_program(g, core, T, topo):
             for a in o["rd"]:
                 rds.setdefault(a[0], []).append((n, a))
 
-    def span(p):
-        return p["cost"] if p["done"] is None else p["done"]
-
-    succ = [[] for _ in ops]
-    left = [0] * len(ops)
-    for n, o in enumerate(ops):
-        o["pre"] = ([(m, span(ops[m]) + LAT) for m in o["hard"]] + [(m, ops[m]["cost"]) for m in o["order"]]
-                    + [(m, d) for m, d in o["soft"]])
-        for m, d in o["pre"]:
-            succ[m].append((n, d))
-        left[n] = len(o["pre"])
-    prio = [0.0] * len(ops)
-    for n in list(range(len(ops) - 1, -1, -1)) * 3:
-        prio[n] = max([span(ops[n])] + [d + prio[k] for k, d in succ[n]])
-        if rank == 0 and ops[n]["sem"] == "remote" and n + 40 < len(ops):
-            prio[n] = max(prio[n + 1:n + 40]) + 500
-    ready = [0.0] * len(ops)
-    free = {}
-    pool = {}
-    for n in range(len(ops)):
-        if left[n] == 0:
-            pool.setdefault(ops[n]["q"], []).append(n)
-    seq = []
-    while len(seq) < len(ops):
-        best = None
-        for q, c in pool.items():
-            if not c:
-                continue
-            t0 = max(free.get(q, 0.0), min(ready[n] for n in c))
-            n = max((k for k in c if ready[k] <= t0 + CFG["slack"]), key=lambda k: (prio[k], -k))
-            t1 = max(t0, ready[n])
-            if best is None or t1 < best[0]:
-                best = (t1, q, n)
-        t1, q, n = best
-        pool[q].remove(n)
-        free[q] = t1 + ops[n]["cost"]
-        seq.append(n)
-        for k, d in succ[n]:
-            ready[k] = max(ready[k], t1 + d)
-            left[k] -= 1
-            if left[k] == 0:
-                pool.setdefault(ops[k]["q"], []).append(k)
+    if "dump" in CFG:
+        CFG["dump"][rank] = (ops, named)
+    seq = arrange(ops, named)
 
     pos = {}
     for n in seq:

from concourse.mybir import AluOpType as ALU, ActivationFunctionType as ACT

N, V, R, L, NT = 4, 1024, 3072, 256, 4
TB = 2048
CR = 327680.0
CFG = {
    "blocks": [(0, 64), (64, 128), (128, 192), (192, 256)],
    "stages": [(0, 128), (128, 192), (192, 256)],
    "gat": [(32 * i, 32 * i + 32) for i in range(8)],
    "old": [(0, 64), (64, 128), (128, 192), (192, 256)],
    "msgs": ["k0", "k1", "k2", "k3m0", "m1m2"],
    "on_s": "g1 g2 key3 so0 so1 so2 mm0 mm1 mo0 mo1 mo2 mo3 dh3 kb dh0 dh1 dh2 fl1 rr1",
    "f32": False,
    "hop": 5500.0, "lat": 270.0, "beta": 20.0, "sc": 3.8, "gam": 1.56, "pe": 0.47, "cy": 0.88, "vfix": 15.0, "sfix": 40.0,
    "kint": True,
    "v": "-st2 -tw2 -w2 -mf1 c0 c1 g0 g3 c2 g4 g5 c3 g7 g6 fl0 sk0 sk1 ki0 ki1 e12 e13 e14 e15 sw0 rr0 ch0 e0 e1 e2 e3 e4 e5 e6 e7 "
         "sk2 st0 tw0 ki2 ch1 sw1 sz0 e8 e9 e10 e11 mu0 st1 w0 sk3 tw1 mf0 sz1 ki3 sz5 sz4 sz3 sz2 mu1 w1 mu2",
    "s": "key3 dh0 kb dh1 mb0 mb1 a5 bf0 mo0 mo1 a6 dh2 a7 thr0 bf1 fl1 mo2 rr2 rr1 thr1 dh3 so0 fl2 kf0 mk0 mm0 so1 kf1 mo3 so2 "
         "mk1 mm1 +g1 +g2 +a0 +a1 +a2 +a3 +a4",
}
WID = 192
EW = 272
LW = 64
LB = LW + 32

SCRATCH = {}
for _dt, _bufs in (
    ("bfloat16", dict(rec_s=R, at_s=L, atb=4 * L, ones=L, ident=128, g1=128, gg=128, gh=128, gn=128, gp=128, gm=128, tz0=128,
                      tz=128, tzh=128, dg=128, bsel=144, ex=2048, dm=WID, cw=WID, cz=WID, ck2=WID, rw=WID, xg=16 * L, ab=16 * L,
                      mb=2 * L, fail=L, rr=L)),
    ("float16", dict(id16=128, id37=128, w16=128, ck=WID, kb=2 * L, dh=L, c16=L, mo16=16)),
    ("int32", dict(ch_s=V, k0_s=16, th_s=4, w_s=4, di=WID, ki=16, ski=L)),
    ("uint16", dict(k0u=16, mi=96, mo=96, coff=L, soff=16)),
    ("float32", dict(id32=128, thf=4, col=4, wf=4, win=TB + 2 * V, iow=2 * V, key3=32, thr=32, rk=WID, rz=WID, bf=L, st=L, tw=L,
                     sw=L, sk=L, sz=L, kf=16, mk=16, mof=16, ykb=L)),
):
    for _k, _n in _bufs.items():
        SCRATCH[_k] = ("sbuf", [128, _n], _dt)
SCRATCH["eq"] = ("sbuf", [128, 16, EW], "bfloat16")
SCRATCH["et"] = ("sbuf", [128, 4, LW], "bfloat16")
SCRATCH["dl"] = ("sbuf", [128, 4, LW], "float32")
SCRATCH["cl"] = ("sbuf", [128, 4, LB], "bfloat16")
SCRATCH["rl"] = ("sbuf", [128, 4, LB], "float32")
SCRATCH["sl"] = ("sbuf", [128, 4, LB], "float32")
PSUM = dict(py=1536, pd0=512, pd1=512, pq=512, pz=512, pl=512)
for _k, _n in PSUM.items():
    SCRATCH[_k] = ("psum", [128, _n], "float32")
SCRATCH["pl"] = ("psum", [128, 4, 128], "float32")
SEMAPHORES = (["qv", "qs", "qt", "qg", "sent", "a0", "a1", "a2", "a3", "k0"]
              + ["%s%d_%d" % (k, s, t) for t in range(NT - 1) for s in range(5) for k in "km"]
              + ["l_at", "l_k0", "l_th", "l_w", "l_ch", "l_c1", "l_r0", "l_r1", "l_hi", "o_c0", "o_c1", "o_k"])


def helper_of(T, topo, r):
    c, nxt = T.cores[r], T.cores[(r + 1) % N]
    ok = [h for h in topo.cores_of(c) if h != c and topo.may_write(h, nxt)]
    near = [h for h in ok if topo.die(h) == topo.die(c)]
    return (near or ok)[0]


def nmask(topo, a, b):
    return len(topo.engines(a, b))


def rsend(g, T, topo, src, dst, out_ap, in_ap, sem):
    rid, pid = topo.addr(dst, src)
    g.remote_dma(out_ap, in_ap, T.sem[sem], T.sem["sent"], pid, rid, topo.mask(src, dst))
    return nmask(topo, src, dst)


def msg_cols(t, m):
    def col(p, end):
        return 32 * t + (0 if p[0] == "k" else 16) + CFG["blocks" if p[0] == "k" else "stages"][int(p[1])][end] // 16
    return col(m[:2], 0), col(m[-2:], 1)


def helper_program(g, core, T, topo, r):
    me = T.cores[r]
    n_in = nmask(topo, me, core)
    sent = 0
    g.wait_ge(T.sem["a0"], n_in)
    sent += rsend(g, T, topo, core, T.cores[(r + 1) % N], T.atb[:, L:2 * L], T.atb[:, 0:L], "a1")
    if not topo.may_write(me, T.cores[0]) and r != 0:
        t = (0 - r) % N
        g.wait_ge(T.sem["k0"], n_in)
        sent += rsend(g, T, topo, core, T.cores[0], T.mi[:, 32 * (t - 1):32 * (t - 1) + 16], T.k0u[:, 0:16], "k0_%d" % (t - 1))
    sent += rsend(g, T, topo, core, T.cores[(r + 3) % N], T.atb[:, 3 * L:4 * L], T.atb[:, 0:L], "a3")
    if r < N - 1:
        for t in range(NT - 1):
            for m in CFG["msgs"]:
                c0, c1 = msg_cols(t, m)
                g.wait_ge(T.sem["%s_%d" % (m[:2], t)], n_in)
                sent += rsend(g, T, topo, core, T.cores[r + 1], T.mi[:, c0:c1], T.mi[:, c0:c1], "%s_%d" % (m[:2], t))
    g.wait_ge(T.sem["sent"], sent)


def arrange(ops, named):
    span = [o["cost"] if o["done"] is None else o["done"] for o in ops]
    succ = [[] for _ in ops]
    left = [0] * len(ops)
    for n, o in enumerate(ops):
        for m, d in ([(m, span[m] + CFG["lat"]) for m in o["hard"]] + [(m, ops[m]["cost"]) for m in o["order"]] + o["soft"]):
            succ[m].append((n, d))
            left[n] += 1
    for q in "vs":
        line = [named.get((t + name.count("+") - name.count("-"), name.strip("+-"))) for t in range(-1, NT + 1)
                for name in CFG[q].split()]
        line = [n for n in line if n is not None and ops[n]["q"] == q]
        for m, n in zip(line, line[1:]):
            succ[m].append((n, ops[m]["cost"]))
            left[n] += 1
    line = [n for n in range(len(ops)) if left[n] == 0]
    pool = {q: [n for n in line if ops[n]["q"] == q] for q in "vstgyx"}
    todo = list(left)
    for n in line:
        for k, d in succ[n]:
            todo[k] -= 1
            if todo[k] == 0:
                line.append(k)
    if len(line) < len(ops):
        return None
    prio = list(span)
    for n in line[::-1]:
        for k, d in succ[n]:
            prio[n] = max(prio[n], d + prio[k])
    ready = [0.0] * len(ops)
    free = {q: 0.0 for q in pool}
    pick, seq = {}, []
    while len(seq) < len(ops):
        for q, c in pool.items():
            if c and q not in pick:
                t0 = max(free[q], min(ready[k] for k in c))
                n = max(c, key=lambda k: (prio[k] - CFG["beta"] * max(0.0, ready[k] - t0), -k))
                pick[q] = (max(t0, ready[n]), n)
        q = min(pick, key=pick.get)
        t1, n = pick.pop(q)
        pool[q].remove(n)
        free[q] = t1 + ops[n]["cost"]
        seq.append(n)
        for k, d in succ[n]:
            ready[k] = max(ready[k], t1 + d)
            left[k] -= 1
            if left[k] == 0:
                pool[ops[k]["q"]].append(k)
                pick.pop(ops[k]["q"], None)
    return seq


def rank_program(g, core, T, topo):
    rank = T.rank_of(core)
    if rank is None:
        for r in range(N):
            if helper_of(T, topo, r) == core:
                helper_program(g, core, T, topo, r)
        return
    BLOCKS, STAGES = CFG["blocks"], CFG["stages"]
    NB, NS = len(BLOCKS), len(STAGES)
    CY, GAM, LAT = CFG["cy"], CFG["gam"], CFG["lat"]
    ON_S = CFG["on_s"].split()
    PARTS = [(STAGES[int(m[m.index("m") + 1])][0], STAGES[int(m[-1])][1], m[-2:]) for m in CFG["msgs"] if "m" in m]
    hlp = helper_of(T, topo, rank)
    ops = []
    sent = [0]
    named = {}
    bank_no = [0]

    def A(name, lo, hi, step=1, p1=128):
        ap = T[name][0:p1, lo:hi:step] if step != 1 else T[name][0:p1, lo:hi]
        return (ap, [(name, lo, hi, step)], (hi - lo + step - 1) // step)

    def B(name, b0, b1, c0, c1):
        w = SCRATCH[name][1][2]
        ap = T[name][:, b0, c0:c1] if b1 == b0 + 1 else T[name][:, b0:b1, c0] if c1 == c0 + 1 else T[name][:, b0:b1, c0:c1]
        return (ap, [(name, w * b + c0, w * b + c1, 1) for b in range(b0, b1)], (b1 - b0) * (c1 - c0))

    def IND(w, o):
        return (w[0].indirect(o[0]), w[1] + o[1], 16 * o[2], w, o)

    def regs(xs):
        out = []
        for x in xs:
            if isinstance(x, tuple):
                out.extend(x[1])
        return out

    def val(x):
        return x[0] if isinstance(x, tuple) else x

    def two(x):
        return SCRATCH[x[1][0][0]][2] in ("bfloat16", "float16", "uint16")

    def add(q, fn, rd, wr, cost, sem=None, done=None):
        ops.append({"q": q, "fn": fn, "rd": regs(rd), "wr": regs(wr), "sem": sem, "inc": False, "cost": cost,
                    "done": done, "soft": [], "name": None})
        return len(ops) - 1

    def vcost(o, i, per=None):
        if len(i) > 3:
            return 50 + i[2] * GAM * CY
        if per is None:
            per = 0.5 if two(o) and two(i) else 1.0
        return CFG["vfix"] + max(64, o[2] * per) * CY

    def vcopy(o, i):
        return add("v", lambda: g.vector.tensor_copy(o[0], i[0]), [i], [o], vcost(o, i))

    def vts(o, i, s1, s2, op0, op1=None):
        if op1 is None:
            return add("v", lambda: g.vector.tensor_scalar(o[0], i[0], val(s1), None, op0), [i, s1], [o], vcost(o, i))
        return add("v", lambda: g.vector.tensor_scalar(o[0], i[0], val(s1), val(s2), op0, op1), [i, s1, s2], [o], vcost(o, i))

    def vtt(o, a, b, op):
        if len(o) > 3:
            return add("v", lambda: g.vector.tensor_tensor(o[0], a[0], b[0], op), [a, b, o[4]], [o[3]], 50 + o[2] * CFG["sc"] * CY)
        per = 1.0 if a[1][0][0] in PSUM or b[1][0][0] in PSUM else 2.0
        return add("v", lambda: g.vector.tensor_tensor(o[0], a[0], b[0], op), [a, b], [o], vcost(o, a, per))

    def vset(o, c):
        return add("v", lambda: g.vector.memset(o[0], c), [], [o], vcost(o, o))

    def vscan(o, d0, d1, init):
        return add("v", lambda: g.vector.tensor_tensor_scan(o[0], d0[0], d1[0], init, ALU.min, ALU.max), [d0, d1], [o],
                   vcost(o, d1, 1.0))

    def act(o, i, f, bias=None, scale=1.0):
        cost = 65 + i[2] * GAM * CY if len(i) > 3 else CFG["sfix"] + i[2] * CY
        if bias is not None:
            return add("s", lambda: g.scalar.activation(o[0], i[0], f, bias=val(bias), scale=scale), [i, bias], [o], cost)
        return add("s", lambda: g.scalar.activation(o[0], i[0], f), [i], [o], cost)

    def lin(e, o, i, scale=1.0, bias=0.0):
        if e == "s":
            return act(o, i, ACT.Identity, bias=bias, scale=scale)
        return vcopy(o, i) if (scale, bias) == (1.0, 0.0) else vts(o, i, scale, bias, ALU.mult, ALU.add)

    def mm(o, lh, rh, start, stop):
        return add("t", lambda: g.tensor.matmul(o[0], lh[0], rh[0], start, stop), [lh, rh], [o],
                   max(min(64, lh[2]), rh[2]) * CFG["pe"] * (1 if two(lh) else 4))

    def group(terms):
        return [mm(o, lh, rh, n == 0, n == len(terms) - 1) for n, (o, lh, rh) in enumerate(terms)]

    def dma(q, o, i, sem, done):
        eng = g.sync if q == "y" else g.scalar
        return add(q, lambda: eng.dma_start(val(o), val(i)), [i], [o], 60, (sem, 16), done)

    def send(dst, out_ap, i, sem):
        sent[0] += nmask(topo, core, dst)
        return add("g", lambda: rsend(g, T, topo, core, dst, out_ap, i[0], sem), [i], [], 300, "remote")

    def M(name):
        return A(name, 0, 128)

    dma("y", A("at_s", 0, L), T.at[:], "l_at", 2200)
    dma("s", A("k0_s", 0, 16), T.key0[:], "l_k0", 2300)
    dma("y", A("ch_s", 0, V // 2), T.ch[:, 0:V // 2], "l_ch", 3800)
    dma("s", A("ch_s", V // 2, V), T.ch[:, V // 2:V], "l_c1", 3800)
    dma("y", A("rec_s", 0, R // 2), T.rec[:, 0:R // 2], "l_r0", 6000)
    dma("s", A("rec_s", R // 2, R), T.rec[:, R // 2:R], "l_r1", 6000)
    dma("y", A("th_s", 0, 1), T.th[:], "l_th", 6500)
    dma("s", A("w_s", 0, 1), T.w[:], "l_w", 6500)
    n_loads = len(ops)

    def sel(o, i, pat, op, base, cm, fill=0.0):
        add("g", lambda: g.affine_select(o[0], i[0], pat, op, fill, base, cm), [i], [o], 170 + 2 * CY * o[2])

    def iota(o, pat, base, cm, small=False):
        if small:
            add("g", lambda: g.iota(o[0], pat, base, cm, allow_small_or_imprecise_dtypes=True), [], [o], 130 + 2 * CY * o[2])
        else:
            add("g", lambda: g.iota(o[0], pat, base, cm), [], [o], 130 + 2 * CY * o[2])

    W = max(l1 - l0 for l0, l1 in STAGES + BLOCKS)
    lw = STAGES[-1][1] - STAGES[-1][0]
    nl = lw // 16
    vset(A("ones", 0, L), 1.0)
    sel(M("ident"), M("ones"), [[-1, 128]], ALU.is_equal, 0, 1)
    sel(M("g1"), M("ones"), [[-16, 8], [0, 16]], ALU.is_ge, 0, 1)
    sel(M("gg"), M("g1"), [[16, 8], [0, 16]], ALU.is_ge, 15, -1)
    iota(A("di", 0, W), [[0, W // 16], [-1, 16]], 16, 1)
    lin("s", M("gn"), M("gg"), -8192.0)
    sel(M("tz0"), M("gn"), [[1, 128]], ALU.is_gt, 0, -1)
    sel(M("tz"), M("tz0"), [[1, 128]], ALU.not_equal, 0, -1, 4096.0)
    vset(A("bsel", 0, 144), 0.0)
    vset(A("rz", 0, W), 4096.0)
    iota(A("rz", 0, W, 16), [[-1, W // 16]], 15, 16, True)
    vset(A("rw", 0, W), 4096.0)
    vset(A("rw", 0, W, 16), 0.0)
    big = float(2 ** 22) if CFG["kint"] else 4096.0
    vset(A("rk", 0, W), big)
    vset(A("rk", 0, W, 16), -big)
    vset(B("rl", 0, nl, 0, LB), -4096.0)
    iota(B("rl", 0, nl, LB - 1, LB), [[1, nl]], 0, 16, True)
    iota(B("dl", 0, nl, 0, LW), [[16, nl], [-1, LW]], 0, 0, True)
    iota(A("iow", 0, V), [[1, V]], 0, 0, True)
    for h in range(2):
        mm(A("pq", 128 * h, 128 * h + 128), A("at_s", 128 * h, 128 * h + 128), M("ident"), True, True)
    for i in range(16):
        lin("sv"[i % 2], A("ex", i, 2048, 16), M("ident"))
    lin("s", A("atb", 0, L), A("pq", 0, L), -1.0)
    vcopy(A("k0u", 0, 16), A("k0_s", 0, 16))
    first = [send(hlp, T.atb[:, 0:L], A("atb", 0, L), "a0")]
    if rank != 0:
        t = (0 - rank) % N
        if topo.may_write(core, T.cores[0]):
            first.append(send(T.cores[0], T.mi[:, 32 * (t - 1):32 * (t - 1) + 16], A("k0u", 0, 16), "k0_%d" % (t - 1)))
        else:
            first.append(send(hlp, T.k0u[:, 0:16], A("k0u", 0, 16), "k0"))
    first.append(send(T.cores[(rank + 2) % N], T.atb[:, 2 * L:3 * L], A("atb", 0, L), "a2"))
    if rank != 0:
        iota(A("iow", V, 2 * V), [[0, V]], V, 0, True)
    vcopy(A("bsel", 15, 128, 16), A("gg", 0, 128, 16))
    vts(A("di", 0, W), A("di", 0, W), 15, None, ALU.bitwise_and)
    vts(A("dm", 0, W), A("di", 0, W), 0.0, None, ALU.is_equal)
    lin("s", A("cw", 0, W), A("dm", 0, W), 2048.0 + 8.0, -2048.0)
    if CFG["kint"]:
        lin("s", A("ck2", 0, W), A("dm", 0, W), float(2 ** 21 + 2 ** 19), -float(2 ** 21))
    else:
        lin("s", A("ck", 0, W), A("dm", 0, W), 2048.0 - 1023.0 / 2048, -2048.0)
    lin("s", A("cz", 0, W), A("dm", 0, W), 16384.0 + TB - 4096.0, -16384.0)
    lin("s", M("id16"), M("ident"))
    lin("s", M("id37"), M("ident"), 37.0)
    lin("s", M("gp"), M("gg"), 4096.0)
    lin("s", M("gm"), M("gg"), -4096.0)
    lin("s", M("tzh"), M("tz"), 0.5)
    lin("s", M("gh"), M("gg"), 0.5)
    lin("v", A("col", 0, 1), A("di", 0, 1))
    lin("v", A("col", 1, 2), A("di", 0, 1), -4096.0, 37 * 2048 + CR - (2048 if CFG["f32"] else 0))
    if CFG["f32"]:
        lin("s", M("id32"), M("ident"))
    vts(M("dg"), M("ident"), A("col", 1, 2), None, ALU.mult)
    vts(B("dl", 0, nl, 0, LW), B("dl", 0, nl, 0, LW), A("col", 0, 1), 0.0, ALU.add, ALU.is_le)
    lin("s", B("cl", 0, nl, 32, LB), B("dl", 0, nl, 0, LW), float(2 ** 19), float(2 ** 18 + 4096 - 65536))
    lin("s", B("cl", 0, nl, 0, 16), A("dm", 0, lw), -float(2 ** 19), float(2 ** 19 + 61440))
    lin("s", B("cl", 0, nl, 16, 32), A("dm", 0, lw), float(TB - 2 ** 22), float(2 ** 22))
    vcopy(A("win", TB, TB + V), A("ch_s", 0, V))
    if rank != 0:
        dma("y", A("win", TB + V, TB + 2 * V), A("win", TB, TB + V), "l_hi", 4000)
    lin("v", A("wf", 0, 1), A("w_s", 0, 1), 1.0 if CFG["kint"] else 1.0 / V)
    lin("v", A("thf", 0, 1), A("th_s", 0, 1), -1.0, -0.5)
    lin("v", A("thf", 1, 2), A("th_s", 0, 1), 1.0, -2048.0)
    lin("v", A("thf", 2, 3), A("th_s", 0, 1), -1.0, 2047.5)
    vts(M("w16"), M("gg"), A("wf", 0, 1), None, ALU.mult)

    def ext(sem, cnt, wr):
        return add("x", None, [], wr, 0, (sem, cnt), 0)

    n_far = nmask(topo, helper_of(T, topo, (rank - 1) % N), core)
    for k, n_ in ((1, n_far), (2, nmask(topo, T.cores[(rank + 2) % N], core)),
                  (3, nmask(topo, helper_of(T, topo, (rank + 1) % N), core))):
        ops[ext("a%d" % k, n_, [A("atb", k * L, k * L + L)])]["soft"].append((first[0], 8000))

    def twin(t, m):
        m = [x for x in CFG["msgs"] if m in x][0]
        return named.get((t, "send " + m), named.get((t, ("dh" if m[-2] == "k" else "so") + m[-1])))

    def arrivals(t):
        if rank == 0:
            b = (0 - (t + 1)) % N
            src = T.cores[b] if topo.may_write(T.cores[b], core) else helper_of(T, topo, b)
            ops[ext("k0_%d" % t, nmask(topo, src, core), [A("mi", 32 * t, 32 * t + 16)])]["soft"].append((first[1], 8000))
        else:
            for m in CFG["msgs"]:
                c0, c1 = msg_cols(t, m)
                n = ext("%s_%d" % (m[:2], t), n_far, [A("mi", c0, c1)])
                ops[n]["soft"].append((twin(t, m), CFG["hop"] + (0 if rank < N - 1 else 1500)))
                ops[n]["name"] = (t, "take " + m)

    TAB = A("win", TB, TB + V)

    def one_round(t):
        fresh = t == 0 or rank == 0
        last = t == NT - 1
        passes = last or rank < N - 1
        sends = []

        def nm(name, n):
            ops[n]["name"] = (t, name)
            named[(t, name)] = n
            return n

        def on(name):
            return "s" if name in ON_S else "v"

        def koff(l0, l1):
            return A("k0u", l0 // 16, l1 // 16) if t == 0 else A("mi", 32 * (t - 1) + l0 // 16, 32 * (t - 1) + l1 // 16)

        def moff(l0, l1):
            return A("mi", 32 * (t - 1) + 16 + l0 // 16, 32 * (t - 1) + 16 + l1 // 16)

        def pd(k, l0, l1):
            return A("pd%d" % ((NB * t + k) % 2), l0, l1)

        def P(name, l0, l1):
            w = SCRATCH[name][1][1] // 2
            return A(name, w * (t % 2) + l0, w * (t % 2) + l1)

        def as_if(n, m):
            if rank == 0 and t > 0:
                ops[n]["soft"].append((twin(t - 1, m), CFG["hop"]))

        for n, (l0, l1) in enumerate(CFG["old"]):
            as_if(nm("c%d" % n, lin(on("c%d" % n), A("coff", l0, l1), IND(A("ch_s", 0, V) if t == 0 else TAB, koff(l0, l1)))),
                  "k%d" % [k for k in range(NB) if BLOCKS[k][0] < l1][-1])
        nm("key3", lin(on("key3"), P("key3", 0, 16), koff(0, L)))
        nm("kb", lin(on("kb"), P("kb", 0, L), IND(A("iow", 0, V), koff(0, L))))
        for s, (l0, l1, m) in enumerate(PARTS):
            if not CFG["f32"]:
                nm("ch%d" % s, lin(on("ch%d" % s), A("c16", l0, l1), A("coff", l0, l1), 1.0, -2047.0))
            if fresh:
                as_if(nm("bf%d" % s, lin("s", A("bf", l0, l1), A("coff", l0, l1))), m)
            else:
                nm("bf%d" % s, lin("s", A("bf", l0, l1), IND(A("win", TB, TB + 2 * V), moff(l0, l1))))
                if passes:
                    nm("thr%d" % s, act(P("thr", l0 // 16, l1 // 16), moff(l0, l1), ACT.Relu, bias=-4096.0 * (V - 1), scale=4096.0))
                nm("mb%d" % s, act(P("mb", l0, l1), IND(A("iow", 0, 2 * V), moff(l0, l1)), ACT.Relu, bias=-float(V - 1)))
        for n, (l0, l1) in enumerate(CFG["gat"]):
            nm("g%d" % n, lin(on("g%d" % n), A("xg", 16 * l0, 16 * l1), IND(A("rec_s", 0, R), A("coff", l0, l1))))

        def block(k):
            l0, l1 = BLOCKS[k]
            b0, b1 = l0 // 16, l1 // 16
            if k == NB - 1:
                nm("fl%d" % (NS - 1), act(A("fail", l0, l1), pd(k, l0, l1), ACT.Sign, bias=A("thf", 0, 1)))
                nm("rr%d" % (NS - 1), lin("s", A("rr", l0, l1), pd(k, l0, l1), -37.0, -(1 - 1023.5 + CR)))
            nm("dh%d" % k, lin(on("dh%d" % k), A("dh", l0, l1), pd(k, l0, l1), 1.0, -2048.0))
            if passes:
                q = pd(k, 256 + l0, 256 + l1)
                mo = A("mo", 32 * (t % 3) + b0, 32 * (t % 3) + b1)
                group([(q, M("ident"), A("ck2", 0, l1 - l0)), (q, M("w16"), A("dh", l0, l1))])
                nm("sk%d" % k, vscan(A("ski", l0, l1), A("rk", 0, l1 - l0), q, 0.0))
                nm("ki%d" % k, vts(A("ki", b0, b1), A("ski", l0 + 15, l1, 16), V - 1, None, ALU.bitwise_and))
                if not last:
                    nm("mo%d" % k, lin(on("mo%d" % k), mo, A("ki", b0, b1)))

        def stage(s):
            l0, l1 = STAGES[s]
            b0, b1 = l0 // 16, l1 // 16
            fin = s == NS - 1
            marked = [] if fresh else [P("mb", l0, l1)]
            fl, rr = "fl%d" % s, "rr%d" % s
            half = fin or on(fl) == "s"
            if not fin:
                if half:
                    nm(fl, act(A("fail", l0, l1), A("dh", l0, l1), ACT.Sign, bias=A("thf", 2, 3)))
                else:
                    nm(fl, vts(A("fail", l0, l1), A("dh", l0, l1), A("thf", 1, 2), 0.5, ALU.is_gt, ALU.subtract))
                nm(rr, lin(on(rr), A("rr", l0, l1), A("dh", l0, l1), -37.0, -(37 * 2048 + 1 - 1023.5 + CR)))
                q = A("pq", l0, l1)
                group([(q, M("ident"), A("cw", 0, l1 - l0))] + [(q, M("ident"), m) for m in marked]
                      + [(q, M("gh" if half else "gg"), A("fail", l0, l1))])
                nm("sw%d" % s, vscan(A("sw", l0, l1), A("rw", 0, l1 - l0), q, 0.0))
            q = A("pq", 256 + l0, 256 + l1)
            base = ([(q, M("ident"), A("ones", l0, l1)), (q, M("id32"), A("bf", l0, l1))] if CFG["f32"]
                    else [(q, M("id16"), A("c16", l0, l1))])
            group([(q, M("dg"), A("ones", l0, l1))] + base + [(q, M("gn"), m) for m in marked]
                  + [(q, M("id37"), A("dh", l0, l1)), (q, M("tzh" if half else "tz"), A("fail", l0, l1)),
                     (q, M("ident"), A("rr", l0, l1))])
            nm("st%d" % s, vtt(A("st", l0, l1), q, A("bf", l0, l1), ALU.max))
            if on("tw%d" % s) == "v":
                nm("tw%d" % s, vts(A("tw", l0, l1), q, float(R), -float(R), ALU.is_ge, ALU.mult))
            else:
                nm("ts%d" % s, act(A("tw", l0, l1), A("st", l0, l1), ACT.Sign, bias=0.5 - R))
                nm("tw%d" % s, lin("s", A("tw", l0, l1), A("tw", l0, l1), -R / 2, -R / 2))
            if not fin:
                z = A("pz", l0, l1)
                for b in range(b0, b1):
                    nm("e%d" % b, vts(B("eq", b, b + 1, 0, L - 16 * b), P("kb", 16 * b, L), P("key3", b, b + 1),
                                      A("sw", 16 * b + 15, 16 * b + 16), ALU.is_equal, ALU.min))
                group([(z, M("ident"), A("cz", 0, l1 - l0)), (z, M("id16"), P("kb", l0, l1))]
                      + [(z, M("gn"), B("eq", b, b + 1, l0 - 16 * b, l1 - 16 * b)) for b in range(b0)]
                      + [(A("pz", 16 * b + 16, l1), M("gn"), B("eq", b, b + 1, 16, l1 - 16 * b)) for b in range(b0, b1 - 1)]
                      + [(z, M("tz"), B("eq", b0, b1, 0, 16))])
                nm("sz%d" % s, vscan(A("sz", l0, l1), A("rz", 0, l1 - l0), z, 4096.0))
                sz = A("sz", l0 + 15, l1, 16)
            else:
                for b in range(nl):
                    nm("e%d" % (b0 + b), vts(B("et", b, b + 1, 0, lw), P("kb", l0, l1), P("key3", b0 + b, b0 + b + 1),
                                             -float(2 ** 18), ALU.is_equal, ALU.mult))
                own, key = B("pl", 0, nl, 0, 16), B("pl", 0, nl, 16, 32)
                terms = [(B("pl", 0, nl, 0, LB), M("ident"), B("cl", 0, nl, 0, LB)), (key, M("id16"), P("kb", l0, l1)),
                         (B("pl", 0, nl, 32, 32 + lw), M("ident"), B("et", 0, nl, 0, lw))]
                for x in marked + [None, A("fail", l0, l1)]:
                    if x is None:
                        terms += [(key, M("gn"), B("eq", b, b + 1, l0 - 16 * b, l1 - 16 * b)) for b in range(b0)]
                    else:
                        terms += [(B("pl", b, b + 1, 32, 32 + lw), M("gm"), x) for b in range(nl)] + [(own, M("gp"), x)]
                group(terms)
                for b in range(nl):
                    n = 48 + 16 * b
                    nm("sz%d" % (s + nl - 1 - b), vscan(B("sl", b, b + 1, LB - n, LB), B("pl", b, b + 1, 0, n),
                                                        B("rl", b, b + 1, LB - n, LB), 4096.0))
                sz = B("sl", 0, nl, LB - 1, LB)
            nm("so%d" % s, lin(on("so%d" % s), A("soff", b0, b1), sz))
            nm("w%d" % s, vtt(IND(A("win", 0, TB + V), A("soff", b0, b1)), A("st", l0, l1), A("tw", l0, l1), ALU.add))
            if passes and not fresh:
                nm("mu%d" % s, vtt(A("mk", b0, b1), sz, P("thr", b0, b1), ALU.add))

        def marks(s, l0, l1):
            b0, b1 = l0 // 16, l1 // 16
            nm("kf%d" % s, lin("s", A("kf", b0, b1), A("ki", b0, b1), 1.0 / 512))
            nm("mk%d" % s, act(A("mk", b0, b1), A("soff" if fresh else "mk", b0, b1), ACT.Sign, bias=0.5 - TB))
            nm("mf%d" % s, vtt(A("mof", b0, b1), A("mk", b0, b1), A("kf", b0, b1), ALU.add))
            nm("mm%d" % s, lin(on("mm%d" % s), A("mo16", b0, b1) if last else A("mo", 32 * t + 16 + b0, 32 * t + 16 + b1),
                               A("mof", b0, b1), 512.0, 512.0))

        for k, (l0, l1) in enumerate(BLOCKS):
            for n, (c0, c1) in enumerate(CFG["gat"]):
                if l0 <= c0 < l1:
                    y0 = 512 * (bank_no[0] % 3)
                    bank_no[0] += 1
                    o = A("py", y0, y0 + 16 * (c1 - c0))
                    y = group([(o, A("atb", L * t + 128 * (c0 // 128), L * t + 128 * (c0 // 128) + 128),
                                A("ex", 16 * (c0 % 128), 16 * (c0 % 128 + c1 - c0))),
                               (o, M("ident"), A("xg", 16 * c0, 16 * c1))])
                    if t > 0 and n < 3:
                        ops[y[0]]["soft"].append((named[(t - 1, "sz%d" % (NS - 1))], 0.0))
                    nm("a%d" % n, act(A("ab", 16 * c0, 16 * c1), o, ACT.Abs))
            group([(pd(k, l0, l1), A("bsel", 15 - i, 143 - i), A("ab", 16 * l0 + i, 16 * l1, 16)) for i in range(16)])
            block(k)
            for s in range(NS):
                if STAGES[s][1] == l1:
                    stage(s)
        if passes:
            for s, (l0, l1, m) in enumerate([(0, L, "")] if last else PARTS):
                marks(len(PARTS) - 1 if last else s, l0, l1)
        if not last:
            if passes:
                for m in CFG["msgs"]:
                    c0, c1 = msg_cols(t, m)
                    nm("send " + m, send(hlp, T.mi[:, c0:c1], A("mo", c0, c1), "%s_%d" % (m[:2], t)))
            arrivals(t)

    for t in range(NT):
        one_round(t)

    dma("y", T.yc[:, 0:V // 2], A("win", TB, TB + V // 2), "o_c0", 3500)
    dma("s", T.yc[:, V // 2:V], A("win", TB + V // 2, TB + V), "o_c1", 3500)
    for a in range(16):
        mm(A("pq", a, L, 16, 8), A("id16", a, 128, 16), A("mo16", 0, 16), True, True)
    vcopy(A("ykb", 0, L, 1, 8), A("pq", 0, L, 1, 8))
    dma("y", T.yk[:], A("ykb", 0, L, 1, 8), "o_k", 2200)

    def exact(a, b):
        if a[1] >= b[2] or b[1] >= a[2]:
            return False
        return not (a[3] == b[3] and (a[1] - b[1]) % a[3] != 0)

    def bank(a, b):
        return a[1] // 512 <= (b[2] - 1) // 512 and b[1] // 512 <= (a[2] - 1) // 512

    wrs, rds = {}, {}
    for n, o in enumerate(ops):
        hard, order = set(), set()
        for a, writes in [(x, False) for x in o["rd"]] + [(x, True) for x in o["wr"]]:
            ps = a[0] in PSUM
            for m, b in wrs.get(a[0], []) + (rds.get(a[0], []) if writes or ps else []):
                p = ops[m]
                if p["q"] == "t" and o["q"] == "t":
                    if ps and bank(a, b):
                        order.add(m)
                elif ps and p["q"] != o["q"]:
                    if bank(a, b):
                        hard.add(m)
                elif exact(a, b) and (writes or b in p["wr"]):
                    hard.add(m)
        if n < n_loads or o["q"] == "g":
            order.update(m for m in range(n) if ops[m]["q"] == o["q"])
        o["hard"], o["order"] = hard, order
        if o["sem"] != "remote":
            for a in o["wr"]:
                for tab in (wrs, rds):
                    if a[0] in PSUM:
                        lo, hi = a[1] // 512 * 512, (a[2] + 511) // 512 * 512
                        tab[a[0]] = [e for e in tab.get(a[0], []) if not (lo <= e[1][1] and e[1][2] <= hi)]
                    elif a[3] == 1:
                        tab[a[0]] = [e for e in tab.get(a[0], []) if not (a[1] <= e[1][1] and e[1][2] <= a[2])]
                wrs.setdefault(a[0], []).append((n, a))
            for a in o["rd"]:
                rds.setdefault(a[0], []).append((n, a))

    if "dump" in CFG:
        CFG["dump"][rank] = (ops, named)
    seq = arrange(ops, named)

    pos = {}
    for n in seq:
        o = ops[n]
        o["key"] = o["q"] if o["sem"] is None or o["sem"] == "remote" else o["sem"][0]
        pos[o["key"]] = pos.get(o["key"], 0) + 1
        o["pos"] = pos[o["key"]]
    seen = {}
    for n in seq:
        o = ops[n]
        known = seen.setdefault(o["q"], {})
        top = {}
        for m in o["hard"]:
            p = ops[m]
            if p["key"] not in top or ops[top[p["key"]]]["pos"] < p["pos"]:
                top[p["key"]] = m
        need = []
        for m in sorted(top.values(), key=lambda k: -len(ops[k]["clock"])):
            p = ops[m]
            if known.get(p["key"], 0) < p["pos"]:
                need.append(m)
                p["inc"] = True
                known[p["key"]] = p["pos"]
                for k_, v_ in p["clock"].items():
                    known[k_] = max(known.get(k_, 0), v_)
        o["need"] = need
        o["clock"] = dict(known)
    count = {}
    for n in seq:
        o = ops[n]
        if o["sem"] is None and o["inc"]:
            count[o["q"]] = count.get(o["q"], 0) + 1
            o["n"] = count[o["q"]]
    queue = {"v": g.vector, "s": g.scalar, "t": g.tensor, "g": g, "y": g.sync}
    for n in seq:
        o = ops[n]
        if o["q"] == "x":
            continue
        for m in o["need"]:
            p = ops[m]
            if p["sem"] is None:
                queue[o["q"]].wait_ge(T.sem["q" + p["q"]], p["n"])
            else:
                queue[o["q"]].wait_ge(T.sem[p["sem"][0]], p["sem"][1])
        ins = o["fn"]()
        if o["sem"] is None:
            if o["inc"]:
                ins.then_inc(T.sem["q" + o["q"]], 1)
        elif o["sem"] != "remote":
            ins.then_inc(T.sem[o["sem"][0]], 16)
    g.wait_ge(T.sem["sent"], sent[0])
    for o in ops:
        if o["sem"] is not None and o["sem"] != "remote" and not o["inc"]:
            g.wait_ge(T.sem[o["sem"][0]], o["sem"][1])
